import numpy as np
import ml_dtypes


def mxq(x, axis, fmt="e4m3"):
    dtype, down = {"e4m3": (ml_dtypes.float8_e4m3fn, 7), "e5m2": (ml_dtypes.float8_e5m2, 14)}[fmt]
    v = np.moveaxis(np.asarray(x, np.float32).astype(ml_dtypes.bfloat16).astype(np.float64), axis, -1)
    blocks = v.reshape(v.shape[:-1] + (-1, 32))
    amax = np.abs(blocks).max(-1, keepdims=True)
    byte = np.maximum(np.where(amax > 0, np.frexp(amax)[1] - 1 + 127, 0) - down, 1)
    scale = np.exp2(byte - 127.0)
    codes = (blocks / scale).astype(np.float32).astype(dtype).astype(np.float64)
    return np.moveaxis((codes * scale).reshape(v.shape), -1, axis)


WIDE = False


def mx_kscale(k):
    if not WIDE:
        return np.ones(k)
    levels = np.array([10, -10, 5, -5, 0])
    if k % 512:
        return np.exp2(np.random.permutation(np.resize(levels, k // 32))).repeat(32)
    a = np.empty((k // 512, 16))
    for p in range(k // 512):
        a[p, :8] = np.random.permutation(np.resize(levels, 8))
        for g in range(8):
            far = levels[np.abs(levels - a[p, g]) >= 10]
            a[p, g + 8] = far[np.random.randint(len(far))]
    return np.exp2(a.ravel()).repeat(32)


def f64(x):
    return np.asarray(x).astype(np.float64)


def striped(idx):
    return np.tile(idx.reshape(-1, 16).T, (8, 1)).astype(np.uint16)


def unstriped(offs):
    return offs[:16].T.reshape(-1).astype(np.int64)


def relu(v):
    return np.maximum(v, 0.0)

def planes(y):
    n, m = y.shape
    v = y.astype(np.float32).astype(ml_dtypes.bfloat16).astype(np.float64).reshape(n // 32, 32, m)
    top = np.abs(v).max(1)
    byte = np.clip(np.where(top > 0, np.frexp(top)[1] - 1 + 127 - 7, 1), 1, 254)
    codes = (v * np.exp2(127.0 - byte)[:, None, :]).reshape(n, m).astype(np.float32).astype(ml_dtypes.float8_e4m3fn).view(np.uint8)
    words = codes.reshape(n // 512, 128, 4, m).transpose(0, 1, 3, 2)
    return np.ascontiguousarray(words), np.ascontiguousarray(byte.astype(np.uint8).reshape(n // 512, 16, m))


K, T, S, N = 512, 1024, 512, 512
P = 2 ** 7


def setup_inputs():
    n = np.random.standard_normal
    s = mx_kscale(K)[:, None]
    return {
        "xT": (n((K, T)) * s).astype(np.float32),
        "gate": np.tile(np.random.uniform(0.2, 1.0, S), (P, 1)).astype(np.float32),
        "res": n((N, T)).astype(np.float32),
        "w1": (n((K, N)) / np.sqrt(K) / s).astype(np.float32),
        "offs": striped(np.random.permutation(T)[:S]),
    }


def reference(xT, gate, res, w1, offs):
    r = f64(res)[:, unstriped(offs)]
    xq = mxq(f64(xT)[:, unstriped(offs)], 0, "e4m3")
    y = relu(mxq(f64(w1), 0, "e4m3").T @ xq)
    out = f64(res).copy()
    out[:, unstriped(offs)] = r + y * f64(gate)[:1]
    return (out,) + planes(out)

@@ -1,0 +1,116 @@
+from contextlib import ExitStack
+
+import concourse.mybir as mybir
+
+K, T, S, N = 512, 1024, 512, 512
+P = 128
+PACK = 4
+HALF_T = T // 2
+HALF_N = N // 2
+ORDER = (2, 0, 1, 3)
+FLOPS = 2 * K * S * N
+
+F32 = mybir.dt.float32
+BF16 = mybir.dt.bfloat16
+I32 = mybir.dt.int32
+U32 = mybir.dt.uint32
+U16 = mybir.dt.uint16
+U8 = mybir.dt.uint8
+FP8X4 = mybir.dt.float8_e4m3fn_x4
+ALU = mybir.AluOpType
+ACT = mybir.ActivationFunctionType
+
+
+def tile_picked_modres_linrelu_lo_kernel(tc, xT, gate, res, w1, offs, out_0, out_1, out_2):
+    nc = tc.nc
+    x_rows = xT.rearrange("(p j) c -> p j c", j=PACK)
+    w_rows = w1.rearrange("(p j) c -> p j c", j=PACK)
+    res_rows = res.rearrange("(p t) c -> p t c", t=PACK)
+    out_rows = out_0.rearrange("(p t) c -> p t c", t=PACK)
+    out_words = out_1.rearrange("z p c r -> p (z c r)").bitcast(I32)
+    out_scales = out_2.rearrange("z q c -> q (z c)").bitcast(I32)
+
+    with ExitStack() as ctx:
+        keep = ctx.enter_context(tc.tile_pool(name="keep", bufs=1))
+        ring = ctx.enter_context(tc.tile_pool(name="ring", bufs=2))
+        psum = ctx.enter_context(tc.psum_pool(name="psum", bufs=1))
+
+        offsets = keep.tile([P, S // 16], U16, name="offsets")
+        nc.sync.dma_start(offsets[:], offs)
+        x_planes = []
+        for j in range(PACK):
+            plane = keep.tile([P, T], F32, name="x_plane%d" % j)
+            nc.sync.dma_start(plane[:], x_rows[:, j, :])
+            x_planes.append(plane)
+        w_halves = []
+        for h in range(2):
+            half = keep.tile([P, PACK, HALF_N], F32, name="w_half%d" % h)
+            nc.sync.dma_start(half[:], w_rows[:, :, h * HALF_N:(h + 1) * HALF_N])
+            w_halves.append(half)
+        windows = [keep.tile([P, T], F32, name="window%d" % t) for t in range(PACK)]
+        gate_sb = keep.tile([P, S], F32, name="gate_sb")
+        nc.sync.dma_start(windows[ORDER[0]][:], res_rows[:, ORDER[0], :])
+        nc.sync.dma_start(gate_sb[:], gate)
+        for t in ORDER[1:]:
+            nc.sync.dma_start(windows[t][:], res_rows[:, t, :])
+
+        x_grouped = keep.tile([P, S, PACK], BF16, name="x_grouped", align_bytes=64)
+        x_pair = keep.tile([P, 2, S], F32, name="x_pair")
+        for j in range(2):
+            nc.vector.tensor_copy(x_pair[:, j, :], x_planes[j][:].indirect(offsets[:]))
+        nc.scalar.copy(x_grouped[:, :, 0:2], x_pair[:].rearrange("p j s -> p s j"))
+        for j in range(2, PACK):
+            nc.vector.tensor_copy(x_grouped[:, :, j], x_planes[j][:].indirect(offsets[:]))
+        x_codes = keep.tile([P, S], U32, name="x_codes", align_bytes=64)
+        x_scales = keep.tile([P, S], U8, name="x_scales", align_bytes=64)
+        nc.vector.quantize_mx(out=x_codes[:].bitcast(FP8X4), scales=x_scales[:], in_=x_grouped[:].rearrange("p s j -> p (s j)"))
+
+        w_grouped = keep.tile([P, PACK, P, PACK], BF16, name="w_grouped", align_bytes=64)
+        for h in range(2):
+            m_half = slice(h * P // 2, (h + 1) * P // 2)
+            nc.scalar.copy(w_grouped[:, :, m_half, :].rearrange("p t m j -> p m j t"),
+                           w_halves[h][:].rearrange("p j (m t) -> p m j t", t=PACK))
+        w_codes = keep.tile([P, PACK, P], U32, name="w_codes", align_bytes=64)
+        w_scales = keep.tile([P, PACK, P], U8, name="w_scales", align_bytes=64)
+
+        out_grouped = [keep.tile([P, HALF_T, PACK], BF16, name="out_grouped%d" % h, align_bytes=64) for h in range(2)]
+        olds = {}
+
+        def look_up_old(t):
+            olds[t] = keep.tile([P, S], F32, name="old%d" % t)
+            nc.vector.tensor_copy(olds[t][:], windows[t][:].indirect(offsets[:]))
+
+        look_up_old(ORDER[0])
+        accs = {}
+        for t in ORDER:
+            nc.vector.quantize_mx(out=w_codes[:, t, :].bitcast(FP8X4), scales=w_scales[:, t, :],
+                                  in_=w_grouped[:, t, :, :].rearrange("p m j -> p (m j)"))
+            accs[t] = psum.tile([P, S], F32, name="acc%d" % t)
+            nc.tensor.matmul_mx(out=accs[t][:], lhsT=w_codes[:, t, :].bitcast(FP8X4), lhsT_scale=w_scales[:, t, :],
+                                rhs=x_codes[:].bitcast(FP8X4), rhs_scale=x_scales[:], start=True, stop=True)
+        for i, t in enumerate(ORDER):
+            act = ring.tile([P, S], F32, name="act")
+            nc.scalar.activation(act[:], accs[t][:], ACT.Relu)
+            gated = keep.tile([P, S], F32, name="gated")
+            nc.vector.tensor_tensor(gated[:], act[:], gate_sb[:], ALU.mult)
+            if i + 1 < PACK:
+                look_up_old(ORDER[i + 1])
+            nc.vector.tensor_tensor(windows[t][:].indirect(offsets[:]), olds[t][:], gated[:], ALU.add)
+            nc.sync.dma_start(out_rows[:, t, :], windows[t][:])
+            for h in range(2):
+                cols = slice(h * HALF_T, (h + 1) * HALF_T)
+                if t == ORDER[-1] and h == 0:
+                    nc.vector.tensor_copy(out_grouped[h][:, :, t], windows[t][:, cols])
+                else:
+                    nc.scalar.copy(out_grouped[h][:, :, t], windows[t][:, cols])
+
+        y_scales = keep.tile([P, T], U8, name="y_scales", align_bytes=64)
+        for h in range(2):
+            cols = slice(h * HALF_T, (h + 1) * HALF_T)
+            y_codes = keep.tile([P, HALF_T], U32, name="y_codes%d" % h, align_bytes=64)
+            nc.vector.quantize_mx(out=y_codes[:].bitcast(FP8X4), scales=y_scales[:, cols],
+                                  in_=out_grouped[h][:].rearrange("p c t -> p (c t)"))
+            nc.sync.dma_start(out_words[:, cols], y_codes[:].bitcast(I32))
+        for q in range(4):
+            queue = nc.scalar if q % 2 else nc.sync
+            queue.dma_start(out_scales[4 * q:4 * q + 4, :], y_scales[32 * q:32 * q + 4, :].bitcast(I32))

@@ -7,7 +7,7 @@ P = 128
 PACK = 4
 HALF_T = T // 2
 HALF_N = N // 2
-ORDER = (2, 0, 1, 3)
+ORDER = (0, 1, 2, 3)
 FLOPS = 2 * K * S * N
 
 F32 = mybir.dt.float32
@@ -32,7 +32,6 @@ def tile_picked_modres_linrelu_lo_kernel(tc, xT, gate, res, w1, offs, out_0, out
 
     with ExitStack() as ctx:
         keep = ctx.enter_context(tc.tile_pool(name="keep", bufs=1))
-        ring = ctx.enter_context(tc.tile_pool(name="ring", bufs=2))
         psum = ctx.enter_context(tc.psum_pool(name="psum", bufs=1))
 
         offsets = keep.tile([P, S // 16], U16, name="offsets")
@@ -49,9 +48,8 @@ def tile_picked_modres_linrelu_lo_kernel(tc, xT, gate, res, w1, offs, out_0, out
             w_halves.append(half)
         windows = [keep.tile([P, T], F32, name="window%d" % t) for t in range(PACK)]
         gate_sb = keep.tile([P, S], F32, name="gate_sb")
-        nc.sync.dma_start(windows[ORDER[0]][:], res_rows[:, ORDER[0], :])
         nc.sync.dma_start(gate_sb[:], gate)
-        for t in ORDER[1:]:
+        for t in ORDER:
             nc.sync.dma_start(windows[t][:], res_rows[:, t, :])
 
         x_grouped = keep.tile([P, S, PACK], BF16, name="x_grouped", align_bytes=64)
@@ -75,32 +73,43 @@ def tile_picked_modres_linrelu_lo_kernel(tc, xT, gate, res, w1, offs, out_0, out
 
         out_grouped = [keep.tile([P, HALF_T, PACK], BF16, name="out_grouped%d" % h, align_bytes=64) for h in range(2)]
         olds = {}
+        accs = {}
+        updates = {}
 
         def look_up_old(t):
             olds[t] = keep.tile([P, S], F32, name="old%d" % t)
             nc.vector.tensor_copy(olds[t][:], windows[t][:].indirect(offsets[:]))
 
-        look_up_old(ORDER[0])
-        accs = {}
-        for t in ORDER:
+        def product(t):
             nc.vector.quantize_mx(out=w_codes[:, t, :].bitcast(FP8X4), scales=w_scales[:, t, :],
                                   in_=w_grouped[:, t, :, :].rearrange("p m j -> p (m j)"))
             accs[t] = psum.tile([P, S], F32, name="acc%d" % t)
             nc.tensor.matmul_mx(out=accs[t][:], lhsT=w_codes[:, t, :].bitcast(FP8X4), lhsT_scale=w_scales[:, t, :],
                                 rhs=x_codes[:].bitcast(FP8X4), rhs_scale=x_scales[:], start=True, stop=True)
-        for i, t in enumerate(ORDER):
-            act = ring.tile([P, S], F32, name="act")
-            nc.scalar.activation(act[:], accs[t][:], ACT.Relu)
+
+        def new_columns(t):
+            updates[t] = keep.tile([P, S], F32, name="update%d" % t)
+            act = keep.tile([P, S], F32, name="act%d" % t)
             gated = keep.tile([P, S], F32, name="gated")
-            nc.vector.tensor_tensor(gated[:], act[:], gate_sb[:], ALU.mult)
-            if i + 1 < PACK:
-                look_up_old(ORDER[i + 1])
-            nc.vector.tensor_tensor(windows[t][:].indirect(offsets[:]), olds[t][:], gated[:], ALU.add)
+            nc.scalar.activation(act[:], accs[t][:], ACT.Relu)
+            nc.gpsimd.tensor_tensor(gated[:], act[:], gate_sb[:], ALU.mult)
+            nc.gpsimd.tensor_tensor(updates[t][:], gated[:], olds[t][:], ALU.add)
+
+        for t in ORDER:
+            product(t)
+        for t in ORDER:
+            look_up_old(t)
+        for t in ORDER:
+            new_columns(t)
+        for i, t in enumerate(ORDER):
+            nc.vector.tensor_copy(windows[t][:].indirect(offsets[:]), updates[t][:])
             nc.sync.dma_start(out_rows[:, t, :], windows[t][:])
             for h in range(2):
                 cols = slice(h * HALF_T, (h + 1) * HALF_T)
                 if t == ORDER[-1] and h == 0:
                     nc.vector.tensor_copy(out_grouped[h][:, :, t], windows[t][:, cols])
+                elif t == ORDER[-2] and h == 0:
+                    nc.scalar.copy(out_grouped[h][:, :, t:t + 2], windows[t][:, cols].unsqueeze(2).to_broadcast([P, HALF_T, 2]))
                 else:
                     nc.scalar.copy(out_grouped[h][:, :, t], windows[t][:, cols])
 

@@ -1,13 +1,14 @@
 from contextlib import ExitStack
 
 import concourse.mybir as mybir
+from concourse.masks import make_identity
 
 K, T, S, N = 512, 1024, 512, 512
 P = 128
 PACK = 4
-HALF_T = T // 2
+SPLIT = 640
 HALF_N = N // 2
-ORDER = (0, 1, 2, 3)
+ORDER = (2, 0, 1, 3)
 FLOPS = 2 * K * S * N
 
 F32 = mybir.dt.float32
@@ -35,12 +36,14 @@ def tile_picked_modres_linrelu_lo_kernel(tc, xT, gate, res, w1, offs, out_0, out
         psum = ctx.enter_context(tc.psum_pool(name="psum", bufs=1))
 
         offsets = keep.tile([P, S // 16], U16, name="offsets")
+        gate_cols = keep.tile([P, PACK], F32, name="gate_cols")
+        x_planes = [keep.tile([P, T], F32, name="x_plane%d" % j) for j in range(PACK)]
+        nc.scalar.dma_start(gate_cols[:], gate[0:1, :].rearrange("o (p c) -> p (o c)", c=PACK))
+        nc.sync.dma_start(x_planes[0][:], x_rows[:, 0, :])
         nc.sync.dma_start(offsets[:], offs)
-        x_planes = []
-        for j in range(PACK):
-            plane = keep.tile([P, T], F32, name="x_plane%d" % j)
-            nc.sync.dma_start(plane[:], x_rows[:, j, :])
-            x_planes.append(plane)
+        nc.sync.dma_start(x_planes[1][:], x_rows[:, 1, :])
+        for j in range(2, PACK):
+            nc.sync.dma_start(x_planes[j][:], x_rows[:, j, :])
         w_halves = []
         for h in range(2):
             half = keep.tile([P, PACK, HALF_N], F32, name="w_half%d" % h)
@@ -48,9 +51,15 @@ def tile_picked_modres_linrelu_lo_kernel(tc, xT, gate, res, w1, offs, out_0, out
             w_halves.append(half)
         windows = [keep.tile([P, T], F32, name="window%d" % t) for t in range(PACK)]
         gate_sb = keep.tile([P, S], F32, name="gate_sb")
-        nc.sync.dma_start(gate_sb[:], gate)
-        for t in ORDER:
+        for t in ORDER[1:] + ORDER[:1]:
             nc.sync.dma_start(windows[t][:], res_rows[:, t, :])
+
+        identity = keep.tile([P, P], F32, name="identity")
+        make_identity(nc, identity[:])
+        gate_ps = psum.tile([P, PACK, P], F32, name="gate_ps")
+        for c in range(PACK):
+            nc.tensor.transpose(gate_ps[:, c, :], gate_cols[:, c:c + 1].to_broadcast([P, P]), identity[:])
+        nc.scalar.copy(gate_sb[:].rearrange("p (n c) -> p n c", c=PACK), gate_ps[:].rearrange("p c n -> p n c"))
 
         x_grouped = keep.tile([P, S, PACK], BF16, name="x_grouped", align_bytes=64)
         x_pair = keep.tile([P, 2, S], F32, name="x_pair")
@@ -63,26 +72,29 @@ def tile_picked_modres_linrelu_lo_kernel(tc, xT, gate, res, w1, offs, out_0, out
         x_scales = keep.tile([P, S], U8, name="x_scales", align_bytes=64)
         nc.vector.quantize_mx(out=x_codes[:].bitcast(FP8X4), scales=x_scales[:], in_=x_grouped[:].rearrange("p s j -> p (s j)"))
 
-        w_grouped = keep.tile([P, PACK, P, PACK], BF16, name="w_grouped", align_bytes=64)
-        for h in range(2):
-            m_half = slice(h * P // 2, (h + 1) * P // 2)
-            nc.scalar.copy(w_grouped[:, :, m_half, :].rearrange("p t m j -> p m j t"),
-                           w_halves[h][:].rearrange("p j (m t) -> p m j t", t=PACK))
+        w_grouped = keep.tile([P, PACK, P, PACK], BF16, name="w_grouped", tag="w_grouped", align_bytes=64)
+        for h, first, last, copy in ((0, 0, 64, nc.scalar.copy), (1, 0, 32, nc.scalar.copy), (1, 32, 64, nc.vector.tensor_copy)):
+            copy(w_grouped[:, :, 64 * h + first:64 * h + last, :].rearrange("p t m j -> p m j t"),
+                 w_halves[h][:].rearrange("p j (m t) -> p m j t", t=PACK)[:, first:last])
         w_codes = keep.tile([P, PACK, P], U32, name="w_codes", align_bytes=64)
         w_scales = keep.tile([P, PACK, P], U8, name="w_scales", align_bytes=64)
 
-        out_grouped = [keep.tile([P, HALF_T, PACK], BF16, name="out_grouped%d" % h, align_bytes=64) for h in range(2)]
+        nc.vector.quantize_mx(out=w_codes[:].rearrange("p t m -> p (t m)").bitcast(FP8X4), scales=w_scales[:].rearrange("p t m -> p (t m)"),
+                              in_=w_grouped[:].rearrange("p t m j -> p (t m j)"))
+
+        out_grouped = keep.tile([P, T, PACK], BF16, name="out_grouped", align_bytes=64)
         olds = {}
         accs = {}
         updates = {}
+        gated = keep.tile([P, S], F32, name="gated")
+        halves = (slice(0, S // 2), slice(S // 2, S))
 
         def look_up_old(t):
-            olds[t] = keep.tile([P, S], F32, name="old%d" % t)
+            tag = "w_grouped" if t == ORDER[1] else "old%d" % t
+            olds[t] = keep.tile([P, S], F32, name="old%d" % t, tag=tag, align_bytes=64)
             nc.vector.tensor_copy(olds[t][:], windows[t][:].indirect(offsets[:]))
 
         def product(t):
-            nc.vector.quantize_mx(out=w_codes[:, t, :].bitcast(FP8X4), scales=w_scales[:, t, :],
-                                  in_=w_grouped[:, t, :, :].rearrange("p m j -> p (m j)"))
             accs[t] = psum.tile([P, S], F32, name="acc%d" % t)
             nc.tensor.matmul_mx(out=accs[t][:], lhsT=w_codes[:, t, :].bitcast(FP8X4), lhsT_scale=w_scales[:, t, :],
                                 rhs=x_codes[:].bitcast(FP8X4), rhs_scale=x_scales[:], start=True, stop=True)
@@ -90,36 +102,40 @@ def tile_picked_modres_linrelu_lo_kernel(tc, xT, gate, res, w1, offs, out_0, out
         def new_columns(t):
             updates[t] = keep.tile([P, S], F32, name="update%d" % t)
             act = keep.tile([P, S], F32, name="act%d" % t)
-            gated = keep.tile([P, S], F32, name="gated")
             nc.scalar.activation(act[:], accs[t][:], ACT.Relu)
-            nc.gpsimd.tensor_tensor(gated[:], act[:], gate_sb[:], ALU.mult)
-            nc.gpsimd.tensor_tensor(updates[t][:], gated[:], olds[t][:], ALU.add)
+            for entries in halves:
+                nc.gpsimd.tensor_tensor(gated[:, entries], act[:, entries], gate_sb[:, entries], ALU.mult)
+            if t == ORDER[0]:
+                nc.vector.tensor_tensor(updates[t][:], windows[t][:].indirect(offsets[:]), gated[:], ALU.add)
+            else:
+                for entries in halves:
+                    nc.gpsimd.tensor_tensor(updates[t][:, entries], gated[:, entries], olds[t][:, entries], ALU.add)
 
         for t in ORDER:
             product(t)
-        for t in ORDER:
+        for t in ORDER[1:]:
             look_up_old(t)
         for t in ORDER:
             new_columns(t)
-        for i, t in enumerate(ORDER):
+        for t in ORDER:
             nc.vector.tensor_copy(windows[t][:].indirect(offsets[:]), updates[t][:])
             nc.sync.dma_start(out_rows[:, t, :], windows[t][:])
-            for h in range(2):
-                cols = slice(h * HALF_T, (h + 1) * HALF_T)
-                if t == ORDER[-1] and h == 0:
-                    nc.vector.tensor_copy(out_grouped[h][:, :, t], windows[t][:, cols])
-                elif t == ORDER[-2] and h == 0:
-                    nc.scalar.copy(out_grouped[h][:, :, t:t + 2], windows[t][:, cols].unsqueeze(2).to_broadcast([P, HALF_T, 2]))
-                else:
-                    nc.scalar.copy(out_grouped[h][:, :, t], windows[t][:, cols])
+            if t < 2:
+                nc.scalar.copy(out_grouped[:, :, t], windows[t][:])
+            elif t == 2:
+                nc.scalar.copy(out_grouped[:, :SPLIT, 2:4], windows[t][:, :SPLIT].unsqueeze(2).to_broadcast([P, SPLIT, 2]))
+                nc.scalar.copy(out_grouped[:, SPLIT:, t], windows[t][:, SPLIT:])
+            else:
+                nc.vector.tensor_copy(out_grouped[:, :512, t], windows[t][:, :512])
+                nc.vector.tensor_copy(out_grouped[:, 512:SPLIT, t], windows[t][:, 512:SPLIT])
+                nc.scalar.copy(out_grouped[:, SPLIT:, t], windows[t][:, SPLIT:])
 
         y_scales = keep.tile([P, T], U8, name="y_scales", align_bytes=64)
-        for h in range(2):
-            cols = slice(h * HALF_T, (h + 1) * HALF_T)
-            y_codes = keep.tile([P, HALF_T], U32, name="y_codes%d" % h, align_bytes=64)
-            nc.vector.quantize_mx(out=y_codes[:].bitcast(FP8X4), scales=y_scales[:, cols],
-                                  in_=out_grouped[h][:].rearrange("p c t -> p (c t)"))
-            nc.sync.dma_start(out_words[:, cols], y_codes[:].bitcast(I32))
+        for first, last in ((0, 512), (512, 768), (768, T)):
+            y_codes = keep.tile([P, last - first], U32, name="y_codes%d" % first, align_bytes=64)
+            nc.vector.quantize_mx(out=y_codes[:].bitcast(FP8X4), scales=y_scales[:, first:last],
+                                  in_=out_grouped[:, first:last, :].rearrange("p c t -> p (c t)"))
+            nc.sync.dma_start(out_words[:, first:last], y_codes[:].bitcast(I32))
         for q in range(4):
             queue = nc.scalar if q % 2 else nc.sync
             queue.dma_start(out_scales[4 * q:4 * q + 4, :], y_scales[32 * q:32 * q + 4, :].bitcast(I32))

@@ -6,10 +6,14 @@ from concourse.masks import make_identity
 K, T, S, N = 512, 1024, 512, 512
 P = 128
 PACK = 4
-SPLIT = 640
-HALF_N = N // 2
-ORDER = (2, 0, 1, 3)
 FLOPS = 2 * K * S * N
+
+SCATTER_ORDER = (0, 2, 3, 1)
+FIRST_PLANE, LAST_PLANE = SCATTER_ORDER[0], SCATTER_ORDER[-1]
+LOAD_ORDER = SCATTER_ORDER[1:] + SCATTER_ORDER[:1]
+W_SHARE = 32
+TAIL_SPLIT = 640
+PLANE_PIECES = ((0, 512), (512, 768), (768, T))
 
 F32 = mybir.dt.float32
 BF16 = mybir.dt.bfloat16
@@ -41,17 +45,15 @@ def tile_picked_modres_linrelu_lo_kernel(tc, xT, gate, res, w1, offs, out_0, out
         nc.scalar.dma_start(gate_cols[:], gate[0:1, :].rearrange("o (p c) -> p (o c)", c=PACK))
         nc.sync.dma_start(x_planes[0][:], x_rows[:, 0, :])
         nc.sync.dma_start(offsets[:], offs)
-        nc.sync.dma_start(x_planes[1][:], x_rows[:, 1, :])
-        for j in range(2, PACK):
+        for j in range(1, PACK):
             nc.sync.dma_start(x_planes[j][:], x_rows[:, j, :])
         w_halves = []
         for h in range(2):
-            half = keep.tile([P, PACK, HALF_N], F32, name="w_half%d" % h)
-            nc.sync.dma_start(half[:], w_rows[:, :, h * HALF_N:(h + 1) * HALF_N])
+            half = keep.tile([P, PACK, N // 2], F32, name="w_half%d" % h, tag="w_half%d" % h)
+            nc.sync.dma_start(half[:], w_rows[:, :, h * N // 2:(h + 1) * N // 2])
             w_halves.append(half)
         windows = [keep.tile([P, T], F32, name="window%d" % t) for t in range(PACK)]
-        gate_sb = keep.tile([P, S], F32, name="gate_sb")
-        for t in ORDER[1:] + ORDER[:1]:
+        for t in LOAD_ORDER:
             nc.sync.dma_start(windows[t][:], res_rows[:, t, :])
 
         identity = keep.tile([P, P], F32, name="identity")
@@ -59,7 +61,6 @@ def tile_picked_modres_linrelu_lo_kernel(tc, xT, gate, res, w1, offs, out_0, out
         gate_ps = psum.tile([P, PACK, P], F32, name="gate_ps")
         for c in range(PACK):
             nc.tensor.transpose(gate_ps[:, c, :], gate_cols[:, c:c + 1].to_broadcast([P, P]), identity[:])
-        nc.scalar.copy(gate_sb[:].rearrange("p (n c) -> p n c", c=PACK), gate_ps[:].rearrange("p c n -> p n c"))
 
         x_grouped = keep.tile([P, S, PACK], BF16, name="x_grouped", align_bytes=64)
         x_pair = keep.tile([P, 2, S], F32, name="x_pair")
@@ -72,70 +73,70 @@ def tile_picked_modres_linrelu_lo_kernel(tc, xT, gate, res, w1, offs, out_0, out
         x_scales = keep.tile([P, S], U8, name="x_scales", align_bytes=64)
         nc.vector.quantize_mx(out=x_codes[:].bitcast(FP8X4), scales=x_scales[:], in_=x_grouped[:].rearrange("p s j -> p (s j)"))
 
-        w_grouped = keep.tile([P, PACK, P, PACK], BF16, name="w_grouped", tag="w_grouped", align_bytes=64)
-        for h, first, last, copy in ((0, 0, 64, nc.scalar.copy), (1, 0, 32, nc.scalar.copy), (1, 32, 64, nc.vector.tensor_copy)):
-            copy(w_grouped[:, :, 64 * h + first:64 * h + last, :].rearrange("p t m j -> p m j t"),
+        w_grouped = keep.tile([P, PACK, P, PACK], BF16, name="w_grouped", align_bytes=64)
+        m_half = P // 2
+        w_copies = ((0, 0, m_half, nc.scalar.copy), (1, 0, W_SHARE, nc.scalar.copy), (1, W_SHARE, m_half, nc.vector.tensor_copy))
+        for h, first, last, copy in w_copies:
+            copy(w_grouped[:, :, m_half * h + first:m_half * h + last, :].rearrange("p t m j -> p m j t"),
                  w_halves[h][:].rearrange("p j (m t) -> p m j t", t=PACK)[:, first:last])
+        gate_sb = keep.tile([P, S], F32, name="gate_sb", tag="w_half1")
+        nc.scalar.copy(gate_sb[:].rearrange("p (n c) -> p n c", c=PACK), gate_ps[:].rearrange("p c n -> p n c"))
         w_codes = keep.tile([P, PACK, P], U32, name="w_codes", align_bytes=64)
         w_scales = keep.tile([P, PACK, P], U8, name="w_scales", align_bytes=64)
+        for t in range(0, PACK, 2):
+            nc.vector.quantize_mx(out=w_codes[:, t:t + 2, :].rearrange("p t m -> p (t m)").bitcast(FP8X4),
+                                  scales=w_scales[:, t:t + 2, :].rearrange("p t m -> p (t m)"),
+                                  in_=w_grouped[:, t:t + 2, :, :].rearrange("p t m j -> p (t m j)"))
 
-        nc.vector.quantize_mx(out=w_codes[:].rearrange("p t m -> p (t m)").bitcast(FP8X4), scales=w_scales[:].rearrange("p t m -> p (t m)"),
-                              in_=w_grouped[:].rearrange("p t m j -> p (t m j)"))
-
-        out_grouped = keep.tile([P, T, PACK], BF16, name="out_grouped", align_bytes=64)
-        olds = {}
-        accs = {}
-        updates = {}
-        gated = keep.tile([P, S], F32, name="gated")
-        halves = (slice(0, S // 2), slice(S // 2, S))
-
-        def look_up_old(t):
-            tag = "w_grouped" if t == ORDER[1] else "old%d" % t
-            olds[t] = keep.tile([P, S], F32, name="old%d" % t, tag=tag, align_bytes=64)
-            nc.vector.tensor_copy(olds[t][:], windows[t][:].indirect(offsets[:]))
-
-        def product(t):
-            accs[t] = psum.tile([P, S], F32, name="acc%d" % t)
-            nc.tensor.matmul_mx(out=accs[t][:], lhsT=w_codes[:, t, :].bitcast(FP8X4), lhsT_scale=w_scales[:, t, :],
+        sums = {}
+        for t in SCATTER_ORDER:
+            sums[t] = psum.tile([P, S], F32, name="sums%d" % t)
+            nc.tensor.matmul_mx(out=sums[t][:], lhsT=w_codes[:, t, :].bitcast(FP8X4), lhsT_scale=w_scales[:, t, :],
                                 rhs=x_codes[:].bitcast(FP8X4), rhs_scale=x_scales[:], start=True, stop=True)
 
-        def new_columns(t):
+        olds = {}
+        for t in SCATTER_ORDER[1:]:
+            olds[t] = keep.tile([P, S], F32, name="old%d" % t)
+            nc.vector.tensor_copy(olds[t][:], windows[t][:].indirect(offsets[:]))
+
+        gated = keep.tile([P, S], F32, name="gated")
+        halves = (slice(0, S // 2), slice(S // 2, S))
+        updates = {}
+        for t in SCATTER_ORDER:
             updates[t] = keep.tile([P, S], F32, name="update%d" % t)
-            act = keep.tile([P, S], F32, name="act%d" % t)
-            nc.scalar.activation(act[:], accs[t][:], ACT.Relu)
+            active = keep.tile([P, S], F32, name="active%d" % t)
+            nc.scalar.activation(active[:], sums[t][:], ACT.Relu)
             for entries in halves:
-                nc.gpsimd.tensor_tensor(gated[:, entries], act[:, entries], gate_sb[:, entries], ALU.mult)
-            if t == ORDER[0]:
+                nc.gpsimd.tensor_tensor(gated[:, entries], active[:, entries], gate_sb[:, entries], ALU.mult)
+            if t == FIRST_PLANE:
                 nc.vector.tensor_tensor(updates[t][:], windows[t][:].indirect(offsets[:]), gated[:], ALU.add)
             else:
                 for entries in halves:
                     nc.gpsimd.tensor_tensor(updates[t][:, entries], gated[:, entries], olds[t][:, entries], ALU.add)
 
-        for t in ORDER:
-            product(t)
-        for t in ORDER[1:]:
-            look_up_old(t)
-        for t in ORDER:
-            new_columns(t)
-        for t in ORDER:
+        out_grouped = keep.tile([P, T, PACK], BF16, name="out_grouped", align_bytes=64)
+        first_piece = PLANE_PIECES[0][1]
+        for t in SCATTER_ORDER:
             nc.vector.tensor_copy(windows[t][:].indirect(offsets[:]), updates[t][:])
             nc.sync.dma_start(out_rows[:, t, :], windows[t][:])
-            if t < 2:
-                nc.scalar.copy(out_grouped[:, :, t], windows[t][:])
-            elif t == 2:
-                nc.scalar.copy(out_grouped[:, :SPLIT, 2:4], windows[t][:, :SPLIT].unsqueeze(2).to_broadcast([P, SPLIT, 2]))
-                nc.scalar.copy(out_grouped[:, SPLIT:, t], windows[t][:, SPLIT:])
+            if t == FIRST_PLANE:
+                nc.scalar.copy(out_grouped[:, :TAIL_SPLIT, 0:2],
+                               windows[t][:, :TAIL_SPLIT].unsqueeze(2).to_broadcast([P, TAIL_SPLIT, 2]))
+                nc.scalar.copy(out_grouped[:, TAIL_SPLIT:, t], windows[t][:, TAIL_SPLIT:])
+            elif t == LAST_PLANE:
+                nc.vector.tensor_copy(out_grouped[:, :first_piece, t], windows[t][:, :first_piece])
+                nc.vector.tensor_copy(out_grouped[:, first_piece:TAIL_SPLIT, t], windows[t][:, first_piece:TAIL_SPLIT])
+                nc.scalar.copy(out_grouped[:, TAIL_SPLIT:, t], windows[t][:, TAIL_SPLIT:])
             else:
-                nc.vector.tensor_copy(out_grouped[:, :512, t], windows[t][:, :512])
-                nc.vector.tensor_copy(out_grouped[:, 512:SPLIT, t], windows[t][:, 512:SPLIT])
-                nc.scalar.copy(out_grouped[:, SPLIT:, t], windows[t][:, SPLIT:])
+                nc.scalar.copy(out_grouped[:, :, t], windows[t][:])
 
         y_scales = keep.tile([P, T], U8, name="y_scales", align_bytes=64)
-        for first, last in ((0, 512), (512, 768), (768, T)):
+        for first, last in PLANE_PIECES:
             y_codes = keep.tile([P, last - first], U32, name="y_codes%d" % first, align_bytes=64)
             nc.vector.quantize_mx(out=y_codes[:].bitcast(FP8X4), scales=y_scales[:, first:last],
                                   in_=out_grouped[:, first:last, :].rearrange("p c t -> p (c t)"))
             nc.sync.dma_start(out_words[:, first:last], y_codes[:].bitcast(I32))
-        for q in range(4):
-            queue = nc.scalar if q % 2 else nc.sync
-            queue.dma_start(out_scales[4 * q:4 * q + 4, :], y_scales[32 * q:32 * q + 4, :].bitcast(I32))
+        for quadrant in range(4):
+            queue = nc.scalar if quadrant % 2 else nc.sync
+            queue.dma_start(out_scales[4 * quadrant:4 * quadrant + 4, :],
+                            y_scales[32 * quadrant:32 * quadrant + 4, :].bitcast(I32))

@@ -11,9 +11,10 @@ FLOPS = 2 * K * S * N
 SCATTER_ORDER = (0, 2, 3, 1)
 FIRST_PLANE, LAST_PLANE = SCATTER_ORDER[0], SCATTER_ORDER[-1]
 LOAD_ORDER = SCATTER_ORDER[1:] + SCATTER_ORDER[:1]
-W_SHARE = 32
-TAIL_SPLIT = 640
-PLANE_PIECES = ((0, 512), (512, 768), (768, T))
+W_SHARE = 28
+TAIL_SPLIT = 512
+POOL_SHARE = 512
+PLANE_PIECES = ((0, 256), (256, 512), (512, 768), (768, T))
 
 F32 = mybir.dt.float32
 BF16 = mybir.dt.bfloat16
@@ -35,6 +36,9 @@ def tile_picked_modres_linrelu_lo_kernel(tc, xT, gate, res, w1, offs, out_0, out
     out_words = out_1.rearrange("z p c r -> p (z c r)").bitcast(I32)
     out_scales = out_2.rearrange("z q c -> q (z c)").bitcast(I32)
 
+    def round_on_gpsimd(out, in_):
+        nc.gpsimd.tensor_scalar(out, in_, 1.0, -0.0, ALU.mult, ALU.add)
+
     with ExitStack() as ctx:
         keep = ctx.enter_context(tc.tile_pool(name="keep", bufs=1))
         psum = ctx.enter_context(tc.psum_pool(name="psum", bufs=1))
@@ -42,18 +46,18 @@ def tile_picked_modres_linrelu_lo_kernel(tc, xT, gate, res, w1, offs, out_0, out
         offsets = keep.tile([P, S // 16], U16, name="offsets")
         gate_cols = keep.tile([P, PACK], F32, name="gate_cols")
         x_planes = [keep.tile([P, T], F32, name="x_plane%d" % j) for j in range(PACK)]
-        nc.scalar.dma_start(gate_cols[:], gate[0:1, :].rearrange("o (p c) -> p (o c)", c=PACK))
-        nc.sync.dma_start(x_planes[0][:], x_rows[:, 0, :])
-        nc.sync.dma_start(offsets[:], offs)
-        for j in range(1, PACK):
-            nc.sync.dma_start(x_planes[j][:], x_rows[:, j, :])
-        w_halves = []
-        for h in range(2):
-            half = keep.tile([P, PACK, N // 2], F32, name="w_half%d" % h, tag="w_half%d" % h)
-            nc.sync.dma_start(half[:], w_rows[:, :, h * N // 2:(h + 1) * N // 2])
-            w_halves.append(half)
         windows = [keep.tile([P, T], F32, name="window%d" % t) for t in range(PACK)]
-        for t in LOAD_ORDER:
+        w_halves = [keep.tile([P, PACK, N // 2], F32, name="w_half%d" % h, tag="w_half%d" % h) for h in range(2)]
+        nc.sync.dma_start(x_planes[1][:], x_rows[:, 1, :])
+        nc.sync.dma_start(offsets[:], offs)
+        nc.sync.dma_start(x_planes[0][:], x_rows[:, 0, :])
+        nc.sync.dma_start(windows[LOAD_ORDER[0]][:], res_rows[:, LOAD_ORDER[0], :])
+        for j in range(2, PACK):
+            nc.sync.dma_start(x_planes[j][:], x_rows[:, j, :])
+        for h in range(2):
+            nc.sync.dma_start(w_halves[h][:], w_rows[:, :, h * N // 2:(h + 1) * N // 2])
+        nc.sync.dma_start(gate_cols[:], gate[0:1, :].rearrange("o (p c) -> p (o c)", c=PACK))
+        for t in LOAD_ORDER[1:]:
             nc.sync.dma_start(windows[t][:], res_rows[:, t, :])
 
         identity = keep.tile([P, P], F32, name="identity")
@@ -63,78 +67,92 @@ def tile_picked_modres_linrelu_lo_kernel(tc, xT, gate, res, w1, offs, out_0, out
             nc.tensor.transpose(gate_ps[:, c, :], gate_cols[:, c:c + 1].to_broadcast([P, P]), identity[:])
 
         x_grouped = keep.tile([P, S, PACK], BF16, name="x_grouped", align_bytes=64)
-        x_pair = keep.tile([P, 2, S], F32, name="x_pair")
-        for j in range(2):
-            nc.vector.tensor_copy(x_pair[:, j, :], x_planes[j][:].indirect(offsets[:]))
-        nc.scalar.copy(x_grouped[:, :, 0:2], x_pair[:].rearrange("p j s -> p s j"))
+        x_picked = keep.tile([P, S], F32, name="x_picked")
+        nc.vector.tensor_copy(x_picked[:], x_planes[1][:].indirect(offsets[:]))
+        x_rounded = keep.tile([P, T], BF16, name="x_rounded")
+        nc.vector.tensor_copy(x_rounded[:], x_planes[0][:])
+        nc.scalar.copy(x_grouped[:, :, 1], x_picked[:])
+        nc.scalar.activation(x_grouped[:, :, 0], x_rounded[:].indirect(offsets[:]), ACT.Copy)
+        olds = {t: keep.tile([P, S], F32, name="old%d" % t) for t in SCATTER_ORDER[1:]}
+        nc.vector.tensor_copy(olds[LOAD_ORDER[0]][:], windows[LOAD_ORDER[0]][:].indirect(offsets[:]))
         for j in range(2, PACK):
             nc.vector.tensor_copy(x_grouped[:, :, j], x_planes[j][:].indirect(offsets[:]))
         x_codes = keep.tile([P, S], U32, name="x_codes", align_bytes=64)
         x_scales = keep.tile([P, S], U8, name="x_scales", align_bytes=64)
         nc.vector.quantize_mx(out=x_codes[:].bitcast(FP8X4), scales=x_scales[:], in_=x_grouped[:].rearrange("p s j -> p (s j)"))
 
-        w_grouped = keep.tile([P, PACK, P, PACK], BF16, name="w_grouped", align_bytes=64)
+        w_grouped = {t: keep.tile([P, 2, P, PACK], BF16, name="w_grouped%d" % t, align_bytes=64) for t in range(0, PACK, 2)}
         m_half = P // 2
-        w_copies = ((0, 0, m_half, nc.scalar.copy), (1, 0, W_SHARE, nc.scalar.copy), (1, W_SHARE, m_half, nc.vector.tensor_copy))
-        for h, first, last, copy in w_copies:
-            copy(w_grouped[:, :, m_half * h + first:m_half * h + last, :].rearrange("p t m j -> p m j t"),
-                 w_halves[h][:].rearrange("p j (m t) -> p m j t", t=PACK)[:, first:last])
+        for h, shares in enumerate((((0, m_half, nc.scalar.copy),),
+                                    ((0, W_SHARE, nc.scalar.copy), (W_SHARE, m_half, nc.vector.tensor_copy)))):
+            for t in range(0, PACK, 2):
+                for first, last, copy in shares:
+                    copy(w_grouped[t][:, :, m_half * h + first:m_half * h + last, :].rearrange("p t m j -> p m j t"),
+                         w_halves[h][:].rearrange("p j (m t) -> p m j t", t=PACK)[:, first:last, :, t:t + 2])
         gate_sb = keep.tile([P, S], F32, name="gate_sb", tag="w_half1")
         nc.scalar.copy(gate_sb[:].rearrange("p (n c) -> p n c", c=PACK), gate_ps[:].rearrange("p c n -> p n c"))
         w_codes = keep.tile([P, PACK, P], U32, name="w_codes", align_bytes=64)
         w_scales = keep.tile([P, PACK, P], U8, name="w_scales", align_bytes=64)
-        for t in range(0, PACK, 2):
-            nc.vector.quantize_mx(out=w_codes[:, t:t + 2, :].rearrange("p t m -> p (t m)").bitcast(FP8X4),
-                                  scales=w_scales[:, t:t + 2, :].rearrange("p t m -> p (t m)"),
-                                  in_=w_grouped[:, t:t + 2, :, :].rearrange("p t m j -> p (t m j)"))
+        for first, last in ((0, 1), (2, 4), (1, 2)):
+            pair = first - first % 2
+            nc.vector.quantize_mx(out=w_codes[:, first:last, :].rearrange("p t m -> p (t m)").bitcast(FP8X4),
+                                  scales=w_scales[:, first:last, :].rearrange("p t m -> p (t m)"),
+                                  in_=w_grouped[pair][:, first - pair:last - pair].rearrange("p t m j -> p (t m j)"))
 
-        sums = {}
+        halves = (slice(0, S // 2), slice(S // 2, S))
+        lead = (slice(0, 128), slice(128, 256), slice(256, S))
+        actives = {}
         for t in SCATTER_ORDER:
-            sums[t] = psum.tile([P, S], F32, name="sums%d" % t)
-            nc.tensor.matmul_mx(out=sums[t][:], lhsT=w_codes[:, t, :].bitcast(FP8X4), lhsT_scale=w_scales[:, t, :],
-                                rhs=x_codes[:].bitcast(FP8X4), rhs_scale=x_scales[:], start=True, stop=True)
+            actives[t] = keep.tile([P, S], F32, name="active%d" % t)
+            for entries in (lead if t == FIRST_PLANE else (slice(0, S),)):
+                sums = psum.tile([P, entries.stop - entries.start], F32, name="sums%d_%d" % (t, entries.start))
+                nc.tensor.matmul_mx(out=sums[:], lhsT=w_codes[:, t, :].bitcast(FP8X4), lhsT_scale=w_scales[:, t, :],
+                                    rhs=x_codes[:, entries].bitcast(FP8X4), rhs_scale=x_scales[:, entries], start=True, stop=True)
+                nc.scalar.activation(actives[t][:, entries], sums[:], ACT.Relu)
 
-        olds = {}
-        for t in SCATTER_ORDER[1:]:
-            olds[t] = keep.tile([P, S], F32, name="old%d" % t)
+        for t in LOAD_ORDER[1:-1]:
             nc.vector.tensor_copy(olds[t][:], windows[t][:].indirect(offsets[:]))
 
         gated = keep.tile([P, S], F32, name="gated")
-        halves = (slice(0, S // 2), slice(S // 2, S))
         updates = {}
         for t in SCATTER_ORDER:
             updates[t] = keep.tile([P, S], F32, name="update%d" % t)
-            active = keep.tile([P, S], F32, name="active%d" % t)
-            nc.scalar.activation(active[:], sums[t][:], ACT.Relu)
-            for entries in halves:
-                nc.gpsimd.tensor_tensor(gated[:, entries], active[:, entries], gate_sb[:, entries], ALU.mult)
+            for entries in ((slice(0, 128), slice(128, S)) if t == FIRST_PLANE else halves):
+                nc.gpsimd.tensor_tensor(gated[:, entries], actives[t][:, entries], gate_sb[:, entries], ALU.mult)
             if t == FIRST_PLANE:
                 nc.vector.tensor_tensor(updates[t][:], windows[t][:].indirect(offsets[:]), gated[:], ALU.add)
             else:
                 for entries in halves:
                     nc.gpsimd.tensor_tensor(updates[t][:, entries], gated[:, entries], olds[t][:, entries], ALU.add)
 
-        out_grouped = keep.tile([P, T, PACK], BF16, name="out_grouped", align_bytes=64)
-        first_piece = PLANE_PIECES[0][1]
+        out_grouped = [keep.tile([P, last - first, PACK], BF16, name="out_grouped%d" % first, align_bytes=64)
+                       for first, last in PLANE_PIECES]
+
+        def round_plane(copy, t, columns, places=1):
+            for (first, last), piece in zip(PLANE_PIECES, out_grouped):
+                begin, end = max(first, columns.start), min(last, columns.stop)
+                if begin < end:
+                    copy(piece[:, begin - first:end - first, t:t + places],
+                         windows[t][:, begin:end].unsqueeze(2).to_broadcast([P, end - begin, places]))
+
         for t in SCATTER_ORDER:
             nc.vector.tensor_copy(windows[t][:].indirect(offsets[:]), updates[t][:])
             nc.sync.dma_start(out_rows[:, t, :], windows[t][:])
-            if t == FIRST_PLANE:
-                nc.scalar.copy(out_grouped[:, :TAIL_SPLIT, 0:2],
-                               windows[t][:, :TAIL_SPLIT].unsqueeze(2).to_broadcast([P, TAIL_SPLIT, 2]))
-                nc.scalar.copy(out_grouped[:, TAIL_SPLIT:, t], windows[t][:, TAIL_SPLIT:])
-            elif t == LAST_PLANE:
-                nc.vector.tensor_copy(out_grouped[:, :first_piece, t], windows[t][:, :first_piece])
-                nc.vector.tensor_copy(out_grouped[:, first_piece:TAIL_SPLIT, t], windows[t][:, first_piece:TAIL_SPLIT])
-                nc.scalar.copy(out_grouped[:, TAIL_SPLIT:, t], windows[t][:, TAIL_SPLIT:])
+            if t < 2:
+                other, theirs, own = nc.vector.tensor_copy, slice(0, TAIL_SPLIT), slice(TAIL_SPLIT, T)
             else:
-                nc.scalar.copy(out_grouped[:, :, t], windows[t][:])
+                other, theirs, own = round_on_gpsimd, slice(T - POOL_SHARE, T), slice(0, T - POOL_SHARE)
+            if t % 2 == 0:
+                round_plane(nc.scalar.copy, t, theirs, places=2)
+            else:
+                round_plane(other, t, theirs)
+            round_plane(nc.scalar.copy, t, own)
 
         y_scales = keep.tile([P, T], U8, name="y_scales", align_bytes=64)
-        for first, last in PLANE_PIECES:
+        for (first, last), piece in zip(PLANE_PIECES, out_grouped):
             y_codes = keep.tile([P, last - first], U32, name="y_codes%d" % first, align_bytes=64)
             nc.vector.quantize_mx(out=y_codes[:].bitcast(FP8X4), scales=y_scales[:, first:last],
-                                  in_=out_grouped[:, first:last, :].rearrange("p c t -> p (c t)"))
+                                  in_=piece[:].rearrange("p c t -> p (c t)"))
             nc.sync.dma_start(out_words[:, first:last], y_codes[:].bitcast(I32))
         for quadrant in range(4):
             queue = nc.scalar if quadrant % 2 else nc.sync

@@ -11,7 +11,7 @@ FLOPS = 2 * K * S * N
 SCATTER_ORDER = (0, 2, 3, 1)
 FIRST_PLANE, LAST_PLANE = SCATTER_ORDER[0], SCATTER_ORDER[-1]
 LOAD_ORDER = SCATTER_ORDER[1:] + SCATTER_ORDER[:1]
-W_SHARE = 28
+W_EARLY = 96
 TAIL_SPLIT = 512
 POOL_SHARE = 512
 PLANE_PIECES = ((0, 256), (256, 512), (512, 768), (768, T))
@@ -47,16 +47,17 @@ def tile_picked_modres_linrelu_lo_kernel(tc, xT, gate, res, w1, offs, out_0, out
         gate_cols = keep.tile([P, PACK], F32, name="gate_cols")
         x_planes = [keep.tile([P, T], F32, name="x_plane%d" % j) for j in range(PACK)]
         windows = [keep.tile([P, T], F32, name="window%d" % t) for t in range(PACK)]
-        w_halves = [keep.tile([P, PACK, N // 2], F32, name="w_half%d" % h, tag="w_half%d" % h) for h in range(2)]
-        nc.sync.dma_start(x_planes[1][:], x_rows[:, 1, :])
-        nc.sync.dma_start(offsets[:], offs)
+        w_ranges = ((0, W_EARLY), (W_EARLY, P))
+        w_parts = [keep.tile([P, PACK, PACK * (last - first)], F32, name="w_part%d" % first, tag="w_part%d" % first) for first, last in w_ranges]
         nc.sync.dma_start(x_planes[0][:], x_rows[:, 0, :])
-        nc.sync.dma_start(windows[LOAD_ORDER[0]][:], res_rows[:, LOAD_ORDER[0], :])
-        for j in range(2, PACK):
+        nc.sync.dma_start(offsets[:], offs)
+        for j in range(1, PACK):
             nc.sync.dma_start(x_planes[j][:], x_rows[:, j, :])
-        for h in range(2):
-            nc.sync.dma_start(w_halves[h][:], w_rows[:, :, h * N // 2:(h + 1) * N // 2])
+        nc.sync.dma_start(w_parts[0][:], w_rows[:, :, 0:PACK * W_EARLY])
         nc.sync.dma_start(gate_cols[:], gate[0:1, :].rearrange("o (p c) -> p (o c)", c=PACK))
+        for t in LOAD_ORDER[:1]:
+            nc.sync.dma_start(windows[t][:], res_rows[:, t, :])
+        nc.sync.dma_start(w_parts[1][:], w_rows[:, :, PACK * W_EARLY:N])
         for t in LOAD_ORDER[1:]:
             nc.sync.dma_start(windows[t][:], res_rows[:, t, :])
 
@@ -67,33 +68,32 @@ def tile_picked_modres_linrelu_lo_kernel(tc, xT, gate, res, w1, offs, out_0, out
             nc.tensor.transpose(gate_ps[:, c, :], gate_cols[:, c:c + 1].to_broadcast([P, P]), identity[:])
 
         x_grouped = keep.tile([P, S, PACK], BF16, name="x_grouped", align_bytes=64)
+        x_rounded = keep.tile([P, T], BF16, name="x_rounded")
+        nc.scalar.copy(x_rounded[:, 0:T // 4], x_planes[0][:, 0:T // 4])
+        nc.vector.tensor_copy(x_rounded[:, T // 4:T], x_planes[0][:, T // 4:T])
+        nc.scalar.activation(x_grouped[:, :, 0], x_rounded[:].indirect(offsets[:]), ACT.Copy)
         x_picked = keep.tile([P, S], F32, name="x_picked")
         nc.vector.tensor_copy(x_picked[:], x_planes[1][:].indirect(offsets[:]))
-        x_rounded = keep.tile([P, T], BF16, name="x_rounded")
-        nc.vector.tensor_copy(x_rounded[:], x_planes[0][:])
         nc.scalar.copy(x_grouped[:, :, 1], x_picked[:])
-        nc.scalar.activation(x_grouped[:, :, 0], x_rounded[:].indirect(offsets[:]), ACT.Copy)
-        olds = {t: keep.tile([P, S], F32, name="old%d" % t) for t in SCATTER_ORDER[1:]}
-        nc.vector.tensor_copy(olds[LOAD_ORDER[0]][:], windows[LOAD_ORDER[0]][:].indirect(offsets[:]))
         for j in range(2, PACK):
             nc.vector.tensor_copy(x_grouped[:, :, j], x_planes[j][:].indirect(offsets[:]))
         x_codes = keep.tile([P, S], U32, name="x_codes", align_bytes=64)
         x_scales = keep.tile([P, S], U8, name="x_scales", align_bytes=64)
         nc.vector.quantize_mx(out=x_codes[:].bitcast(FP8X4), scales=x_scales[:], in_=x_grouped[:].rearrange("p s j -> p (s j)"))
+        olds = {t: keep.tile([P, S], F32, name="old%d" % t) for t in SCATTER_ORDER[1:]}
+        for t in LOAD_ORDER[:1]:
+            nc.vector.tensor_copy(olds[t][:], windows[t][:].indirect(offsets[:]))
 
         w_grouped = {t: keep.tile([P, 2, P, PACK], BF16, name="w_grouped%d" % t, align_bytes=64) for t in range(0, PACK, 2)}
-        m_half = P // 2
-        for h, shares in enumerate((((0, m_half, nc.scalar.copy),),
-                                    ((0, W_SHARE, nc.scalar.copy), (W_SHARE, m_half, nc.vector.tensor_copy)))):
-            for t in range(0, PACK, 2):
-                for first, last, copy in shares:
-                    copy(w_grouped[t][:, :, m_half * h + first:m_half * h + last, :].rearrange("p t m j -> p m j t"),
-                         w_halves[h][:].rearrange("p j (m t) -> p m j t", t=PACK)[:, first:last, :, t:t + 2])
-        gate_sb = keep.tile([P, S], F32, name="gate_sb", tag="w_half1")
+        for (first, last), part, copies in zip(w_ranges, w_parts, ((nc.scalar.copy, nc.scalar.copy), (nc.scalar.copy, nc.scalar.copy))):
+            for t, copy in zip(range(0, PACK, 2), copies):
+                copy(w_grouped[t][:, :, first:last, :].rearrange("p t m j -> p m j t"),
+                     part[:].rearrange("p j (m t) -> p m j t", t=PACK)[:, :, :, t:t + 2])
+        gate_sb = keep.tile([P, S], F32, name="gate_sb", tag="w_part%d" % W_EARLY)
         nc.scalar.copy(gate_sb[:].rearrange("p (n c) -> p n c", c=PACK), gate_ps[:].rearrange("p c n -> p n c"))
         w_codes = keep.tile([P, PACK, P], U32, name="w_codes", align_bytes=64)
         w_scales = keep.tile([P, PACK, P], U8, name="w_scales", align_bytes=64)
-        for first, last in ((0, 1), (2, 4), (1, 2)):
+        for first, last in ((0, 1), (1, 2), (2, 4)):
             pair = first - first % 2
             nc.vector.quantize_mx(out=w_codes[:, first:last, :].rearrange("p t m -> p (t m)").bitcast(FP8X4),
                                   scales=w_scales[:, first:last, :].rearrange("p t m -> p (t m)"),
@@ -117,7 +117,7 @@ def tile_picked_modres_linrelu_lo_kernel(tc, xT, gate, res, w1, offs, out_0, out
         updates = {}
         for t in SCATTER_ORDER:
             updates[t] = keep.tile([P, S], F32, name="update%d" % t)
-            for entries in ((slice(0, 128), slice(128, S)) if t == FIRST_PLANE else halves):
+            for entries in (lead if t == FIRST_PLANE else halves):
                 nc.gpsimd.tensor_tensor(gated[:, entries], actives[t][:, entries], gate_sb[:, entries], ALU.mult)
             if t == FIRST_PLANE:
                 nc.vector.tensor_tensor(updates[t][:], windows[t][:].indirect(offsets[:]), gated[:], ALU.add)

@@ -15,6 +15,7 @@ W_EARLY = 96
 TAIL_SPLIT = 512
 POOL_SHARE = 512
 PLANE_PIECES = ((0, 256), (256, 512), (512, 768), (768, T))
+DMA_ALIGN = 256
 
 F32 = mybir.dt.float32
 BF16 = mybir.dt.bfloat16
@@ -45,10 +46,10 @@ def tile_picked_modres_linrelu_lo_kernel(tc, xT, gate, res, w1, offs, out_0, out
 
         offsets = keep.tile([P, S // 16], U16, name="offsets")
         gate_cols = keep.tile([P, PACK], F32, name="gate_cols")
-        x_planes = [keep.tile([P, T], F32, name="x_plane%d" % j) for j in range(PACK)]
-        windows = [keep.tile([P, T], F32, name="window%d" % t) for t in range(PACK)]
+        x_planes = [keep.tile([P, T], F32, name="x_plane%d" % j, align_bytes=DMA_ALIGN) for j in range(PACK)]
+        windows = [keep.tile([P, T], F32, name="window%d" % t, align_bytes=DMA_ALIGN) for t in range(PACK)]
         w_ranges = ((0, W_EARLY), (W_EARLY, P))
-        w_parts = [keep.tile([P, PACK, PACK * (last - first)], F32, name="w_part%d" % first, tag="w_part%d" % first) for first, last in w_ranges]
+        w_parts = [keep.tile([P, PACK, PACK * (last - first)], F32, name="w_part%d" % first, tag="w_part%d" % first, align_bytes=DMA_ALIGN) for first, last in w_ranges]
         nc.sync.dma_start(x_planes[0][:], x_rows[:, 0, :])
         nc.sync.dma_start(offsets[:], offs)
         for j in range(1, PACK):
@@ -89,7 +90,7 @@ def tile_picked_modres_linrelu_lo_kernel(tc, xT, gate, res, w1, offs, out_0, out
             for t, copy in zip(range(0, PACK, 2), copies):
                 copy(w_grouped[t][:, :, first:last, :].rearrange("p t m j -> p m j t"),
                      part[:].rearrange("p j (m t) -> p m j t", t=PACK)[:, :, :, t:t + 2])
-        gate_sb = keep.tile([P, S], F32, name="gate_sb", tag="w_part%d" % W_EARLY)
+        gate_sb = keep.tile([P, S], F32, name="gate_sb", tag="w_part%d" % W_EARLY, align_bytes=DMA_ALIGN)
         nc.scalar.copy(gate_sb[:].rearrange("p (n c) -> p n c", c=PACK), gate_ps[:].rearrange("p c n -> p n c"))
         w_codes = keep.tile([P, PACK, P], U32, name="w_codes", align_bytes=64)
         w_scales = keep.tile([P, PACK, P], U8, name="w_scales", align_bytes=64)
@@ -148,9 +149,9 @@ def tile_picked_modres_linrelu_lo_kernel(tc, xT, gate, res, w1, offs, out_0, out
                 round_plane(other, t, theirs)
             round_plane(nc.scalar.copy, t, own)
 
-        y_scales = keep.tile([P, T], U8, name="y_scales", align_bytes=64)
+        y_scales = keep.tile([P, T], U8, name="y_scales", align_bytes=DMA_ALIGN)
         for (first, last), piece in zip(PLANE_PIECES, out_grouped):
-            y_codes = keep.tile([P, last - first], U32, name="y_codes%d" % first, align_bytes=64)
+            y_codes = keep.tile([P, last - first], U32, name="y_codes%d" % first, align_bytes=DMA_ALIGN)
             nc.vector.quantize_mx(out=y_codes[:].bitcast(FP8X4), scales=y_scales[:, first:last],
                                   in_=piece[:].rearrange("p c t -> p (c t)"))
             nc.sync.dma_start(out_words[:, first:last], y_codes[:].bitcast(I32))

@@ -52,7 +52,7 @@ def tile_picked_modres_linrelu_lo_kernel(tc, xT, gate, res, w1, offs, out_0, out
         w_parts = [keep.tile([P, PACK, PACK * (last - first)], F32, name="w_part%d" % first, tag="w_part%d" % first, align_bytes=DMA_ALIGN) for first, last in w_ranges]
         nc.sync.dma_start(x_planes[0][:], x_rows[:, 0, :])
         nc.sync.dma_start(offsets[:], offs)
-        for j in range(1, PACK):
+        for j in (2, 1, 3):
             nc.sync.dma_start(x_planes[j][:], x_rows[:, j, :])
         nc.sync.dma_start(w_parts[0][:], w_rows[:, :, 0:PACK * W_EARLY])
         nc.sync.dma_start(gate_cols[:], gate[0:1, :].rearrange("o (p c) -> p (o c)", c=PACK))
@@ -69,13 +69,12 @@ def tile_picked_modres_linrelu_lo_kernel(tc, xT, gate, res, w1, offs, out_0, out
             nc.tensor.transpose(gate_ps[:, c, :], gate_cols[:, c:c + 1].to_broadcast([P, P]), identity[:])
 
         x_grouped = keep.tile([P, S, PACK], BF16, name="x_grouped", align_bytes=64)
-        x_rounded = keep.tile([P, T], BF16, name="x_rounded")
-        nc.scalar.copy(x_rounded[:, 0:T // 4], x_planes[0][:, 0:T // 4])
-        nc.vector.tensor_copy(x_rounded[:, T // 4:T], x_planes[0][:, T // 4:T])
-        nc.scalar.activation(x_grouped[:, :, 0], x_rounded[:].indirect(offsets[:]), ACT.Copy)
-        x_picked = keep.tile([P, S], F32, name="x_picked")
-        nc.vector.tensor_copy(x_picked[:], x_planes[1][:].indirect(offsets[:]))
-        nc.scalar.copy(x_grouped[:, :, 1], x_picked[:])
+        x_rounded = [keep.tile([P, T], BF16, name="x_rounded%d" % j) for j in range(2)]
+        nc.scalar.copy(x_rounded[0][:, 0:T // 2], x_planes[0][:, 0:T // 2])
+        nc.vector.tensor_copy(x_rounded[0][:, T // 2:T], x_planes[0][:, T // 2:T])
+        nc.vector.tensor_copy(x_rounded[1][:], x_planes[1][:])
+        for j in range(2):
+            nc.scalar.activation(x_grouped[:, :, j], x_rounded[j][:].indirect(offsets[:]), ACT.Copy)
         for j in range(2, PACK):
             nc.vector.tensor_copy(x_grouped[:, :, j], x_planes[j][:].indirect(offsets[:]))
         x_codes = keep.tile([P, S], U32, name="x_codes", align_bytes=64)

@@ -70,10 +70,9 @@ def tile_picked_modres_linrelu_lo_kernel(tc, xT, gate, res, w1, offs, out_0, out
 
         x_grouped = keep.tile([P, S, PACK], BF16, name="x_grouped", align_bytes=64)
         x_rounded = [keep.tile([P, T], BF16, name="x_rounded%d" % j) for j in range(2)]
-        nc.scalar.copy(x_rounded[0][:, 0:T // 2], x_planes[0][:, 0:T // 2])
-        nc.vector.tensor_copy(x_rounded[0][:, T // 2:T], x_planes[0][:, T // 2:T])
-        nc.vector.tensor_copy(x_rounded[1][:], x_planes[1][:])
         for j in range(2):
+            nc.scalar.copy(x_rounded[j][:, 0:T // 2], x_planes[j][:, 0:T // 2])
+            nc.vector.tensor_copy(x_rounded[j][:, T // 2:T], x_planes[j][:, T // 2:T])
             nc.scalar.activation(x_grouped[:, :, j], x_rounded[j][:].indirect(offsets[:]), ACT.Copy)
         for j in range(2, PACK):
             nc.vector.tensor_copy(x_grouped[:, :, j], x_planes[j][:].indirect(offsets[:]))
@@ -93,7 +92,7 @@ def tile_picked_modres_linrelu_lo_kernel(tc, xT, gate, res, w1, offs, out_0, out
         nc.scalar.copy(gate_sb[:].rearrange("p (n c) -> p n c", c=PACK), gate_ps[:].rearrange("p c n -> p n c"))
         w_codes = keep.tile([P, PACK, P], U32, name="w_codes", align_bytes=64)
         w_scales = keep.tile([P, PACK, P], U8, name="w_scales", align_bytes=64)
-        for first, last in ((0, 1), (1, 2), (2, 4)):
+        for first, last in ((0, 2), (2, 4)):
             pair = first - first % 2
             nc.vector.quantize_mx(out=w_codes[:, first:last, :].rearrange("p t m -> p (t m)").bitcast(FP8X4),
                                   scales=w_scales[:, first:last, :].rearrange("p t m -> p (t m)"),
@@ -120,7 +119,9 @@ def tile_picked_modres_linrelu_lo_kernel(tc, xT, gate, res, w1, offs, out_0, out
             for entries in (lead if t == FIRST_PLANE else halves):
                 nc.gpsimd.tensor_tensor(gated[:, entries], actives[t][:, entries], gate_sb[:, entries], ALU.mult)
             if t == FIRST_PLANE:
-                nc.vector.tensor_tensor(updates[t][:], windows[t][:].indirect(offsets[:]), gated[:], ALU.add)
+                for entries in halves:
+                    nc.vector.tensor_tensor(updates[t][:, entries], windows[t][:].indirect(offsets[:, entries.start // 16:entries.stop // 16]),
+                                            gated[:, entries], ALU.add)
             else:
                 for entries in halves:
                     nc.gpsimd.tensor_tensor(updates[t][:, entries], gated[:, entries], olds[t][:, entries], ALU.add)
@@ -154,7 +155,6 @@ def tile_picked_modres_linrelu_lo_kernel(tc, xT, gate, res, w1, offs, out_0, out
             nc.vector.quantize_mx(out=y_codes[:].bitcast(FP8X4), scales=y_scales[:, first:last],
                                   in_=piece[:].rearrange("p c t -> p (c t)"))
             nc.sync.dma_start(out_words[:, first:last], y_codes[:].bitcast(I32))
-        for quadrant in range(4):
-            queue = nc.scalar if quadrant % 2 else nc.sync
-            queue.dma_start(out_scales[4 * quadrant:4 * quadrant + 4, :],
-                            y_scales[32 * quadrant:32 * quadrant + 4, :].bitcast(I32))
+        for row in range(4):
+            queue = nc.scalar if row % 2 else nc.sync
+            queue.dma_start(out_scales[row:16:4, :], y_scales[row:P:32, :].bitcast(I32))

@@ -8,13 +8,10 @@ P = 128
 PACK = 4
 FLOPS = 2 * K * S * N
 
-SCATTER_ORDER = (0, 2, 3, 1)
-FIRST_PLANE, LAST_PLANE = SCATTER_ORDER[0], SCATTER_ORDER[-1]
-LOAD_ORDER = SCATTER_ORDER[1:] + SCATTER_ORDER[:1]
-W_EARLY = 96
-TAIL_SPLIT = 512
-POOL_SHARE = 512
-PLANE_PIECES = ((0, 256), (256, 512), (512, 768), (768, T))
+RES_ORDER = (0, 2, 3, 1)
+W_EARLY = 64
+X_SPLIT = 352
+PIECE = 256
 DMA_ALIGN = 256
 
 F32 = mybir.dt.float32
@@ -36,15 +33,17 @@ def tile_picked_modres_linrelu_lo_kernel(tc, xT, gate, res, w1, offs, out_0, out
     out_rows = out_0.rearrange("(p t) c -> p t c", t=PACK)
     out_words = out_1.rearrange("z p c r -> p (z c r)").bitcast(I32)
     out_scales = out_2.rearrange("z q c -> q (z c)").bitcast(I32)
-
-    def round_on_gpsimd(out, in_):
-        nc.gpsimd.tensor_scalar(out, in_, 1.0, -0.0, ALU.mult, ALU.add)
+    halves = (slice(0, S // 2), slice(S // 2, S))
 
     with ExitStack() as ctx:
         keep = ctx.enter_context(tc.tile_pool(name="keep", bufs=1))
         psum = ctx.enter_context(tc.psum_pool(name="psum", bufs=1))
 
         offsets = keep.tile([P, S // 16], U16, name="offsets")
+
+        def picked(window, entries):
+            return window[:].indirect(offsets[:, entries.start // 16:entries.stop // 16])
+
         gate_cols = keep.tile([P, PACK], F32, name="gate_cols")
         x_planes = [keep.tile([P, T], F32, name="x_plane%d" % j, align_bytes=DMA_ALIGN) for j in range(PACK)]
         windows = [keep.tile([P, T], F32, name="window%d" % t, align_bytes=DMA_ALIGN) for t in range(PACK)]
@@ -52,14 +51,12 @@ def tile_picked_modres_linrelu_lo_kernel(tc, xT, gate, res, w1, offs, out_0, out
         w_parts = [keep.tile([P, PACK, PACK * (last - first)], F32, name="w_part%d" % first, tag="w_part%d" % first, align_bytes=DMA_ALIGN) for first, last in w_ranges]
         nc.sync.dma_start(x_planes[0][:], x_rows[:, 0, :])
         nc.sync.dma_start(offsets[:], offs)
-        for j in (2, 1, 3):
+        for j in range(1, PACK):
             nc.sync.dma_start(x_planes[j][:], x_rows[:, j, :])
         nc.sync.dma_start(w_parts[0][:], w_rows[:, :, 0:PACK * W_EARLY])
         nc.sync.dma_start(gate_cols[:], gate[0:1, :].rearrange("o (p c) -> p (o c)", c=PACK))
-        for t in LOAD_ORDER[:1]:
-            nc.sync.dma_start(windows[t][:], res_rows[:, t, :])
         nc.sync.dma_start(w_parts[1][:], w_rows[:, :, PACK * W_EARLY:N])
-        for t in LOAD_ORDER[1:]:
+        for t in RES_ORDER:
             nc.sync.dma_start(windows[t][:], res_rows[:, t, :])
 
         identity = keep.tile([P, P], F32, name="identity")
@@ -69,92 +66,82 @@ def tile_picked_modres_linrelu_lo_kernel(tc, xT, gate, res, w1, offs, out_0, out
             nc.tensor.transpose(gate_ps[:, c, :], gate_cols[:, c:c + 1].to_broadcast([P, P]), identity[:])
 
         x_grouped = keep.tile([P, S, PACK], BF16, name="x_grouped", align_bytes=64)
-        x_rounded = [keep.tile([P, T], BF16, name="x_rounded%d" % j) for j in range(2)]
-        for j in range(2):
-            nc.scalar.copy(x_rounded[j][:, 0:T // 2], x_planes[j][:, 0:T // 2])
-            nc.vector.tensor_copy(x_rounded[j][:, T // 2:T], x_planes[j][:, T // 2:T])
-            nc.scalar.activation(x_grouped[:, :, j], x_rounded[j][:].indirect(offsets[:]), ACT.Copy)
-        for j in range(2, PACK):
-            nc.vector.tensor_copy(x_grouped[:, :, j], x_planes[j][:].indirect(offsets[:]))
+        x_plain = keep.tile([P, PACK, S], BF16, name="x_plain", align_bytes=64)
+        nc.scalar.activation(x_plain[:, 0, :], picked(x_planes[0], slice(0, S)), ACT.Copy)
+        for j in (1, 2):
+            nc.vector.tensor_copy(x_plain[:, j, :], picked(x_planes[j], slice(0, S)))
+        nc.vector.tensor_copy(x_plain[:, 3, halves[0]], picked(x_planes[3], halves[0]))
+        nc.scalar.activation(x_plain[:, 3, halves[1]], picked(x_planes[3], halves[1]), ACT.Copy)
+        for entries, copy in ((slice(0, X_SPLIT), nc.vector.tensor_copy), (slice(X_SPLIT, S), nc.scalar.copy)):
+            copy(x_grouped[:, entries, :].rearrange("p (c i) j -> p c j i", i=4),
+                 x_plain[:, :, entries].rearrange("p j (c i) -> p c j i", i=4))
         x_codes = keep.tile([P, S], U32, name="x_codes", align_bytes=64)
         x_scales = keep.tile([P, S], U8, name="x_scales", align_bytes=64)
         nc.vector.quantize_mx(out=x_codes[:].bitcast(FP8X4), scales=x_scales[:], in_=x_grouped[:].rearrange("p s j -> p (s j)"))
-        olds = {t: keep.tile([P, S], F32, name="old%d" % t) for t in SCATTER_ORDER[1:]}
-        for t in LOAD_ORDER[:1]:
-            nc.vector.tensor_copy(olds[t][:], windows[t][:].indirect(offsets[:]))
 
-        w_grouped = {t: keep.tile([P, 2, P, PACK], BF16, name="w_grouped%d" % t, align_bytes=64) for t in range(0, PACK, 2)}
-        for (first, last), part, copies in zip(w_ranges, w_parts, ((nc.scalar.copy, nc.scalar.copy), (nc.scalar.copy, nc.scalar.copy))):
-            for t, copy in zip(range(0, PACK, 2), copies):
-                copy(w_grouped[t][:, :, first:last, :].rearrange("p t m j -> p m j t"),
-                     part[:].rearrange("p j (m t) -> p m j t", t=PACK)[:, :, :, t:t + 2])
-        gate_sb = keep.tile([P, S], F32, name="gate_sb", tag="w_part%d" % W_EARLY, align_bytes=DMA_ALIGN)
-        nc.scalar.copy(gate_sb[:].rearrange("p (n c) -> p n c", c=PACK), gate_ps[:].rearrange("p c n -> p n c"))
         w_codes = keep.tile([P, PACK, P], U32, name="w_codes", align_bytes=64)
         w_scales = keep.tile([P, PACK, P], U8, name="w_scales", align_bytes=64)
-        for first, last in ((0, 2), (2, 4)):
-            pair = first - first % 2
-            nc.vector.quantize_mx(out=w_codes[:, first:last, :].rearrange("p t m -> p (t m)").bitcast(FP8X4),
-                                  scales=w_scales[:, first:last, :].rearrange("p t m -> p (t m)"),
-                                  in_=w_grouped[pair][:, first - pair:last - pair].rearrange("p t m j -> p (t m j)"))
+        w_grouped = {t: keep.tile([P, 2, P, PACK], BF16, name="w_grouped%d" % t, align_bytes=64) for t in (0, 2)}
+        for (first, last), part in zip(w_ranges, w_parts):
+            for t, copy in ((0, nc.vector.tensor_copy), (2, nc.scalar.copy)):
+                copy(w_grouped[t][:, :, first:last, :].rearrange("p t m j -> p m j t"),
+                     part[:].rearrange("p j (m t) -> p m j t", t=PACK)[:, :, :, t:t + 2])
+        for t in (0, 2):
+            nc.vector.quantize_mx(out=w_codes[:, t:t + 2, :].rearrange("p t m -> p (t m)").bitcast(FP8X4),
+                                  scales=w_scales[:, t:t + 2, :].rearrange("p t m -> p (t m)"),
+                                  in_=w_grouped[t][:].rearrange("p t m j -> p (t m j)"))
+        gate_sb = keep.tile([P, S], F32, name="gate_sb", tag="w_part%d" % W_EARLY, align_bytes=DMA_ALIGN)
+        nc.scalar.copy(gate_sb[:].rearrange("p (n c) -> p n c", c=PACK), gate_ps[:].rearrange("p c n -> p n c"))
 
-        halves = (slice(0, S // 2), slice(S // 2, S))
-        lead = (slice(0, 128), slice(128, 256), slice(256, S))
-        actives = {}
-        for t in SCATTER_ORDER:
-            actives[t] = keep.tile([P, S], F32, name="active%d" % t)
-            for entries in (lead if t == FIRST_PLANE else (slice(0, S),)):
-                sums = psum.tile([P, entries.stop - entries.start], F32, name="sums%d_%d" % (t, entries.start))
-                nc.tensor.matmul_mx(out=sums[:], lhsT=w_codes[:, t, :].bitcast(FP8X4), lhsT_scale=w_scales[:, t, :],
-                                    rhs=x_codes[:, entries].bitcast(FP8X4), rhs_scale=x_scales[:, entries], start=True, stop=True)
-                nc.scalar.activation(actives[t][:, entries], sums[:], ACT.Relu)
+        gated = {}
+        for t in range(PACK):
+            sums = psum.tile([P, S], F32, name="sums%d" % t)
+            nc.tensor.matmul_mx(out=sums[:], lhsT=w_codes[:, t, :].bitcast(FP8X4), lhsT_scale=w_scales[:, t, :],
+                                rhs=x_codes[:].bitcast(FP8X4), rhs_scale=x_scales[:], start=True, stop=True)
+            gated[t] = keep.tile([P, S], F32, name="gated%d" % t, tag="gated%d" % t, align_bytes=64)
+            nc.vector.scalar_tensor_tensor(gated[t][:], sums[:], 0.0, gate_sb[:], ALU.max, ALU.mult)
 
-        for t in LOAD_ORDER[1:-1]:
-            nc.vector.tensor_copy(olds[t][:], windows[t][:].indirect(offsets[:]))
+        olds = {}
+        for t in RES_ORDER:
+            olds[t] = keep.tile([P, S], F32, name="old%d" % t, tag="old%d" % t, align_bytes=64)
+            for entries in (halves if t == 1 else (slice(0, S),)):
+                nc.scalar.activation(olds[t][:, entries], picked(windows[t], entries), ACT.Copy)
 
-        gated = keep.tile([P, S], F32, name="gated")
         updates = {}
-        for t in SCATTER_ORDER:
-            updates[t] = keep.tile([P, S], F32, name="update%d" % t)
-            for entries in (lead if t == FIRST_PLANE else halves):
-                nc.gpsimd.tensor_tensor(gated[:, entries], actives[t][:, entries], gate_sb[:, entries], ALU.mult)
-            if t == FIRST_PLANE:
-                for entries in halves:
-                    nc.vector.tensor_tensor(updates[t][:, entries], windows[t][:].indirect(offsets[:, entries.start // 16:entries.stop // 16]),
-                                            gated[:, entries], ALU.add)
-            else:
-                for entries in halves:
-                    nc.gpsimd.tensor_tensor(updates[t][:, entries], gated[:, entries], olds[t][:, entries], ALU.add)
+        for t in (0, 2, 1, 3):
+            updates[t] = keep.tile([P, S], F32, name="update%d" % t, tag="gated1" if t == 3 else "update%d" % t, align_bytes=64)
+            for entries in (halves if t == 1 else (slice(0, S),)):
+                nc.gpsimd.tensor_tensor(updates[t][:, entries], gated[t][:, entries], olds[t][:, entries], ALU.add)
 
-        out_grouped = [keep.tile([P, last - first, PACK], BF16, name="out_grouped%d" % first, align_bytes=64)
-                       for first, last in PLANE_PIECES]
-
-        def round_plane(copy, t, columns, places=1):
-            for (first, last), piece in zip(PLANE_PIECES, out_grouped):
-                begin, end = max(first, columns.start), min(last, columns.stop)
-                if begin < end:
-                    copy(piece[:, begin - first:end - first, t:t + places],
-                         windows[t][:, begin:end].unsqueeze(2).to_broadcast([P, end - begin, places]))
-
-        for t in SCATTER_ORDER:
-            nc.vector.tensor_copy(windows[t][:].indirect(offsets[:]), updates[t][:])
-            nc.sync.dma_start(out_rows[:, t, :], windows[t][:])
-            if t < 2:
-                other, theirs, own = nc.vector.tensor_copy, slice(0, TAIL_SPLIT), slice(TAIL_SPLIT, T)
-            else:
-                other, theirs, own = round_on_gpsimd, slice(T - POOL_SHARE, T), slice(0, T - POOL_SHARE)
+        sides = (slice(0, T // 2), slice(T // 2, T))
+        pairs = [keep.tile([P, 2, T // 2, 2], BF16, name="pairs%d" % n, tag=tag, align_bytes=64) for n, tag in enumerate(("gated3", "old3"))]
+        for t in range(PACK):
             if t % 2 == 0:
-                round_plane(nc.scalar.copy, t, theirs, places=2)
+                nc.vector.tensor_copy(picked(windows[t], slice(0, S)), updates[t][:])
             else:
-                round_plane(other, t, theirs)
-            round_plane(nc.scalar.copy, t, own)
+                for entries in halves:
+                    nc.scalar.activation(picked(windows[t], entries), updates[t][:, entries], ACT.Copy)
+            nc.sync.dma_start(out_rows[:, t, :], windows[t][:])
+            for side, pair in zip(sides, pairs):
+                if t < 2:
+                    nc.gpsimd.tensor_scalar(pair[:, 0, :, t], windows[t][:, side], 1.0, -0.0, ALU.mult, ALU.add)
+                else:
+                    nc.vector.tensor_copy(pair[:, 1, :, t - 2], windows[t][:, side])
 
+        pieces = [slice(first, first + PIECE) for first in range(0, T, PIECE)]
         y_scales = keep.tile([P, T], U8, name="y_scales", align_bytes=DMA_ALIGN)
-        for (first, last), piece in zip(PLANE_PIECES, out_grouped):
-            y_codes = keep.tile([P, last - first], U32, name="y_codes%d" % first, align_bytes=DMA_ALIGN)
-            nc.vector.quantize_mx(out=y_codes[:].bitcast(FP8X4), scales=y_scales[:, first:last],
-                                  in_=piece[:].rearrange("p c t -> p (c t)"))
-            nc.sync.dma_start(out_words[:, first:last], y_codes[:].bitcast(I32))
+        groups = []
+        for n, piece in enumerate(pieces):
+            grouped = keep.tile([P, PIECE * PACK], BF16, name="out_grouped%d" % n, align_bytes=64)
+            groups.append(grouped)
+            copy, word = (nc.vector.tensor_copy, I32) if n == len(pieces) - 1 else (nc.scalar.copy, U32)
+            side, first = divmod(piece.start, T // 2)
+            words = pairs[side][:].rearrange("p u c e -> p (u c e)").bitcast(word).rearrange("p (u c) -> p c u", u=2)
+            copy(grouped[:].bitcast(word).rearrange("p (c u) -> p c u", u=2), words[:, first:first + PIECE, :])
+        for n in (0, 3, 1, 2):
+            y_codes = keep.tile([P, PIECE], U32, name="y_codes%d" % n, align_bytes=DMA_ALIGN)
+            nc.vector.quantize_mx(out=y_codes[:].bitcast(FP8X4), scales=y_scales[:, pieces[n]], in_=groups[n][:])
+            nc.sync.dma_start(out_words[:, pieces[n]], y_codes[:].bitcast(I32))
         for row in range(4):
             queue = nc.scalar if row % 2 else nc.sync
             queue.dma_start(out_scales[row:16:4, :], y_scales[row:P:32, :].bitcast(I32))

@@ -11,6 +11,7 @@ FLOPS = 2 * K * S * N
 RES_ORDER = (0, 2, 3, 1)
 W_EARLY = 64
 X_SPLIT = 352
+BETWEEN = 128
 PIECE = 256
 DMA_ALIGN = 256
 
@@ -59,6 +60,10 @@ def tile_picked_modres_linrelu_lo_kernel(tc, xT, gate, res, w1, offs, out_0, out
         for t in RES_ORDER:
             nc.sync.dma_start(windows[t][:], res_rows[:, t, :])
 
+        warm_in = keep.tile([P, 1], F32, name="warm_in")
+        warm_out = keep.tile([P, 1], F32, name="warm_out")
+        nc.vector.memset(warm_in[:], 0.0)
+        nc.scalar.activation(warm_out[:], warm_in[:], ACT.Copy)
         identity = keep.tile([P, P], F32, name="identity")
         make_identity(nc, identity[:])
         gate_ps = psum.tile([P, PACK, P], F32, name="gate_ps")
@@ -66,61 +71,71 @@ def tile_picked_modres_linrelu_lo_kernel(tc, xT, gate, res, w1, offs, out_0, out
             nc.tensor.transpose(gate_ps[:, c, :], gate_cols[:, c:c + 1].to_broadcast([P, P]), identity[:])
 
         x_grouped = keep.tile([P, S, PACK], BF16, name="x_grouped", align_bytes=64)
-        x_plain = keep.tile([P, PACK, S], BF16, name="x_plain", align_bytes=64)
-        nc.scalar.activation(x_plain[:, 0, :], picked(x_planes[0], slice(0, S)), ACT.Copy)
-        for j in (1, 2):
-            nc.vector.tensor_copy(x_plain[:, j, :], picked(x_planes[j], slice(0, S)))
-        nc.vector.tensor_copy(x_plain[:, 3, halves[0]], picked(x_planes[3], halves[0]))
-        nc.scalar.activation(x_plain[:, 3, halves[1]], picked(x_planes[3], halves[1]), ACT.Copy)
+        x_plain = [keep.tile([P, 2, S], BF16, name="x_plain%d" % u, align_bytes=64) for u in range(2)]
+        whole = slice(0, S)
+        nc.scalar.activation(x_plain[0][:, 0, :], picked(x_planes[0], whole), ACT.Copy)
+        nc.vector.tensor_copy(x_plain[0][:, 1, :], picked(x_planes[1], whole))
+        nc.scalar.activation(x_plain[1][:, 0, :], picked(x_planes[2], whole), ACT.Copy)
+        nc.vector.tensor_copy(x_grouped[:, :, 0:2], x_plain[0][:].rearrange("p j s -> p s j"))
+        nc.vector.tensor_copy(x_plain[1][:, 1, halves[0]], picked(x_planes[3], halves[0]))
+        nc.scalar.activation(x_plain[1][:, 1, halves[1]], picked(x_planes[3], halves[1]), ACT.Copy)
         for entries, copy in ((slice(0, X_SPLIT), nc.vector.tensor_copy), (slice(X_SPLIT, S), nc.scalar.copy)):
-            copy(x_grouped[:, entries, :].rearrange("p (c i) j -> p c j i", i=4),
-                 x_plain[:, :, entries].rearrange("p j (c i) -> p c j i", i=4))
+            copy(x_grouped[:, entries, 2:PACK], x_plain[1][:, :, entries].rearrange("p j s -> p s j"))
         x_codes = keep.tile([P, S], U32, name="x_codes", align_bytes=64)
         x_scales = keep.tile([P, S], U8, name="x_scales", align_bytes=64)
         nc.vector.quantize_mx(out=x_codes[:].bitcast(FP8X4), scales=x_scales[:], in_=x_grouped[:].rearrange("p s j -> p (s j)"))
 
-        w_codes = keep.tile([P, PACK, P], U32, name="w_codes", align_bytes=64)
-        w_scales = keep.tile([P, PACK, P], U8, name="w_scales", align_bytes=64)
-        w_grouped = {t: keep.tile([P, 2, P, PACK], BF16, name="w_grouped%d" % t, align_bytes=64) for t in (0, 2)}
-        for (first, last), part in zip(w_ranges, w_parts):
-            for t, copy in ((0, nc.vector.tensor_copy), (2, nc.scalar.copy)):
-                copy(w_grouped[t][:, :, first:last, :].rearrange("p t m j -> p m j t"),
-                     part[:].rearrange("p j (m t) -> p m j t", t=PACK)[:, :, :, t:t + 2])
-        for t in (0, 2):
-            nc.vector.quantize_mx(out=w_codes[:, t:t + 2, :].rearrange("p t m -> p (t m)").bitcast(FP8X4),
-                                  scales=w_scales[:, t:t + 2, :].rearrange("p t m -> p (t m)"),
+        w_codes = {t: keep.tile([P, 2 * P], U32, name="w_codes%d" % t, align_bytes=64) for t in (0, 1)}
+        w_scales = {t: keep.tile([P, 2 * P], U8, name="w_scales%d" % t, align_bytes=64) for t in (0, 1)}
+        w_grouped = {t: keep.tile([P, 2, P, PACK], BF16, name="w_grouped%d" % t, tag="w_grouped%d" % t, align_bytes=64) for t in (0, 1)}
+        for part, t, copy in ((0, 0, nc.scalar.copy), (0, 1, nc.vector.tensor_copy), (1, 0, nc.scalar.copy), (1, 1, nc.scalar.copy)):
+            first, last = w_ranges[part]
+            copy(w_grouped[t][:, :, first:last, :].rearrange("p t m j -> p m j t"),
+                 w_parts[part][:].rearrange("p j (m t) -> p m j t", t=PACK)[:, :, :, t:PACK:2])
+        for t in (0, 1):
+            nc.vector.quantize_mx(out=w_codes[t][:].bitcast(FP8X4), scales=w_scales[t][:],
                                   in_=w_grouped[t][:].rearrange("p t m j -> p (t m j)"))
-        gate_sb = keep.tile([P, S], F32, name="gate_sb", tag="w_part%d" % W_EARLY, align_bytes=DMA_ALIGN)
-        nc.scalar.copy(gate_sb[:].rearrange("p (n c) -> p n c", c=PACK), gate_ps[:].rearrange("p c n -> p n c"))
+            if t == 0:
+                gate_sb = keep.tile([P, S], F32, name="gate_sb", tag="w_grouped0", align_bytes=64)
+                nc.vector.tensor_copy(gate_sb[:].rearrange("p (n c) -> p n c", c=PACK), gate_ps[:].rearrange("p c n -> p n c"))
 
         gated = {}
-        for t in range(PACK):
+        for t in (0, 2, 1, 3):
             sums = psum.tile([P, S], F32, name="sums%d" % t)
-            nc.tensor.matmul_mx(out=sums[:], lhsT=w_codes[:, t, :].bitcast(FP8X4), lhsT_scale=w_scales[:, t, :],
+            pair, columns = t % 2, slice(t // 2 * P, (t // 2 + 1) * P)
+            nc.tensor.matmul_mx(out=sums[:], lhsT=w_codes[pair][:, columns].bitcast(FP8X4), lhsT_scale=w_scales[pair][:, columns],
                                 rhs=x_codes[:].bitcast(FP8X4), rhs_scale=x_scales[:], start=True, stop=True)
             gated[t] = keep.tile([P, S], F32, name="gated%d" % t, tag="gated%d" % t, align_bytes=64)
             nc.vector.scalar_tensor_tensor(gated[t][:], sums[:], 0.0, gate_sb[:], ALU.max, ALU.mult)
 
-        olds = {}
-        for t in RES_ORDER:
-            olds[t] = keep.tile([P, S], F32, name="old%d" % t, tag="old%d" % t, align_bytes=64)
-            for entries in (halves if t == 1 else (slice(0, S),)):
-                nc.scalar.activation(olds[t][:, entries], picked(windows[t], entries), ACT.Copy)
+        early, late = halves
+        updates = {t: keep.tile([P, S], F32, name="update%d" % t, align_bytes=64) for t in range(PACK)}
+        old0 = keep.tile([P, S], F32, name="old0")
+        old2 = keep.tile([P, S // 2], F32, name="old2")
+        old3 = keep.tile([P, S], F32, name="old3", tag="old3", align_bytes=64)
+        olds = {(2, 0): old2[:], (2, 1): updates[3][:, late], (3, 0): old3[:, early], (3, 1): old3[:, late],
+                (1, 0): updates[3][:, early], (1, 1): updates[2][:, late]}
+        nc.scalar.activation(old0[:], picked(windows[0], whole), ACT.Copy)
+        for t in RES_ORDER[1:]:
+            for half, entries in enumerate(halves):
+                if (t, half) == (3, 0):
+                    nc.vector.tensor_copy(olds[t, half], picked(windows[t], entries))
+                else:
+                    nc.scalar.activation(olds[t, half], picked(windows[t], entries), ACT.Copy)
+        between, rest = slice(0, BETWEEN), slice(BETWEEN, S)
+        nc.gpsimd.tensor_tensor(updates[0][:], gated[0][:], old0[:], ALU.add)
+        for t, entries, old in ((2, early, olds[2, 0]), (1, early, olds[1, 0]), (3, between, old3[:, between]),
+                                (1, late, olds[1, 1]), (2, late, olds[2, 1]), (3, rest, old3[:, rest])):
+            nc.gpsimd.tensor_tensor(updates[t][:, entries], gated[t][:, entries], old, ALU.add)
 
-        updates = {}
-        for t in (0, 2, 1, 3):
-            updates[t] = keep.tile([P, S], F32, name="update%d" % t, tag="gated1" if t == 3 else "update%d" % t, align_bytes=64)
-            for entries in (halves if t == 1 else (slice(0, S),)):
-                nc.gpsimd.tensor_tensor(updates[t][:, entries], gated[t][:, entries], olds[t][:, entries], ALU.add)
+        nc.vector.tensor_copy(picked(windows[0], whole), updates[0][:])
+        for t, entries in ((1, early), (3, between), (1, late), (3, rest)):
+            nc.scalar.activation(picked(windows[t], entries), updates[t][:, entries], ACT.Copy)
+        nc.vector.tensor_copy(picked(windows[2], whole), updates[2][:])
 
         sides = (slice(0, T // 2), slice(T // 2, T))
         pairs = [keep.tile([P, 2, T // 2, 2], BF16, name="pairs%d" % n, tag=tag, align_bytes=64) for n, tag in enumerate(("gated3", "old3"))]
         for t in range(PACK):
-            if t % 2 == 0:
-                nc.vector.tensor_copy(picked(windows[t], slice(0, S)), updates[t][:])
-            else:
-                for entries in halves:
-                    nc.scalar.activation(picked(windows[t], entries), updates[t][:, entries], ACT.Copy)
             nc.sync.dma_start(out_rows[:, t, :], windows[t][:])
             for side, pair in zip(sides, pairs):
                 if t < 2:

@@ -133,30 +133,38 @@ def tile_picked_modres_linrelu_lo_kernel(tc, xT, gate, res, w1, offs, out_0, out
             nc.scalar.activation(picked(windows[t], entries), updates[t][:, entries], ACT.Copy)
         nc.vector.tensor_copy(picked(windows[2], whole), updates[2][:])
 
-        sides = (slice(0, T // 2), slice(T // 2, T))
-        pairs = [keep.tile([P, 2, T // 2, 2], BF16, name="pairs%d" % n, tag=tag, align_bytes=64) for n, tag in enumerate(("gated3", "old3"))]
+        sides = (slice(0, PIECE), slice(PIECE, T))
+        pairs = [keep.tile([P, 2, side.stop - side.start, 2], BF16, name="pairs_" + tag, tag=tag, align_bytes=64)
+                 for side, tag in zip(sides, ("gated3", "old3"))]
         for t in range(PACK):
             nc.sync.dma_start(out_rows[:, t, :], windows[t][:])
             for side, pair in zip(sides, pairs):
-                if t < 2:
+                if t < 2 and side.start:
                     nc.gpsimd.tensor_scalar(pair[:, 0, :, t], windows[t][:, side], 1.0, -0.0, ALU.mult, ALU.add)
                 else:
-                    nc.vector.tensor_copy(pair[:, 1, :, t - 2], windows[t][:, side])
+                    nc.vector.tensor_copy(pair[:, t // 2, :, t % 2], windows[t][:, side])
 
         pieces = [slice(first, first + PIECE) for first in range(0, T, PIECE)]
         y_scales = keep.tile([P, T], U8, name="y_scales", align_bytes=DMA_ALIGN)
-        groups = []
-        for n, piece in enumerate(pieces):
-            grouped = keep.tile([P, PIECE * PACK], BF16, name="out_grouped%d" % n, align_bytes=64)
-            groups.append(grouped)
-            copy, word = (nc.vector.tensor_copy, I32) if n == len(pieces) - 1 else (nc.scalar.copy, U32)
-            side, first = divmod(piece.start, T // 2)
+        groups = [keep.tile([P, PIECE * PACK], BF16, name="out_grouped%d" % n, align_bytes=64) for n in range(len(pieces))]
+
+        def weave(n, copy, word):
+            side = min(n, 1)
+            first = pieces[n].start - sides[side].start
             words = pairs[side][:].rearrange("p u c e -> p (u c e)").bitcast(word).rearrange("p (u c) -> p c u", u=2)
-            copy(grouped[:].bitcast(word).rearrange("p (c u) -> p c u", u=2), words[:, first:first + PIECE, :])
-        for n in (0, 3, 1, 2):
+            copy(groups[n][:].bitcast(word).rearrange("p (c u) -> p c u", u=2), words[:, first:first + PIECE, :])
+
+        def quantise(n):
             y_codes = keep.tile([P, PIECE], U32, name="y_codes%d" % n, align_bytes=DMA_ALIGN)
             nc.vector.quantize_mx(out=y_codes[:].bitcast(FP8X4), scales=y_scales[:, pieces[n]], in_=groups[n][:])
             nc.sync.dma_start(out_words[:, pieces[n]], y_codes[:].bitcast(I32))
+
+        for n in range(3):
+            weave(n, nc.scalar.copy, U32)
+        quantise(0)
+        weave(3, nc.vector.tensor_copy, I32)
+        for n in (1, 3, 2):
+            quantise(n)
         for row in range(4):
             queue = nc.scalar if row % 2 else nc.sync
             queue.dma_start(out_scales[row:16:4, :], y_scales[row:P:32, :].bitcast(I32))

@@ -109,7 +109,7 @@ def tile_picked_modres_linrelu_lo_kernel(tc, xT, gate, res, w1, offs, out_0, out
             nc.vector.scalar_tensor_tensor(gated[t][:], sums[:], 0.0, gate_sb[:], ALU.max, ALU.mult)
 
         early, late = halves
-        updates = {t: keep.tile([P, S], F32, name="update%d" % t, align_bytes=64) for t in range(PACK)}
+        updates = {t: keep.tile([P, S], F32, name="update%d" % t, tag="update%d" % t, align_bytes=64) for t in range(PACK)}
         old0 = keep.tile([P, S], F32, name="old0")
         old2 = keep.tile([P, S // 2], F32, name="old2")
         old3 = keep.tile([P, S], F32, name="old3", tag="old3", align_bytes=64)
@@ -135,7 +135,7 @@ def tile_picked_modres_linrelu_lo_kernel(tc, xT, gate, res, w1, offs, out_0, out
 
         sides = (slice(0, PIECE), slice(PIECE, T))
         pairs = [keep.tile([P, 2, side.stop - side.start, 2], BF16, name="pairs_" + tag, tag=tag, align_bytes=64)
-                 for side, tag in zip(sides, ("gated3", "old3"))]
+                 for side, tag in zip(sides, ("update2", "old3"))]
         for t in range(PACK):
             nc.sync.dma_start(out_rows[:, t, :], windows[t][:])
             for side, pair in zip(sides, pairs):

@@ -1,18 +1,19 @@
 from contextlib import ExitStack
 
 import concourse.mybir as mybir
-from concourse.masks import make_identity
 
 K, T, S, N = 512, 1024, 512, 512
 P = 128
 PACK = 4
+QUAD = 32
 FLOPS = 2 * K * S * N
 
-RES_ORDER = (0, 2, 3, 1)
-W_EARLY = 64
-X_SPLIT = 352
-BETWEEN = 128
-PIECE = 256
+PLANE_ORDER = (0, 2, 3, 1)
+X_SPLIT = 320
+SHARE = 128
+BLOCK = 64
+VECTOR_PIECES = (slice(0, 6), slice(6, 10))
+SCALAR_PIECES = (slice(10, 14), slice(14, 16))
 DMA_ALIGN = 256
 
 F32 = mybir.dt.float32
@@ -34,7 +35,8 @@ def tile_picked_modres_linrelu_lo_kernel(tc, xT, gate, res, w1, offs, out_0, out
     out_rows = out_0.rearrange("(p t) c -> p t c", t=PACK)
     out_words = out_1.rearrange("z p c r -> p (z c r)").bitcast(I32)
     out_scales = out_2.rearrange("z q c -> q (z c)").bitcast(I32)
-    halves = (slice(0, S // 2), slice(S // 2, S))
+    whole = slice(0, S)
+    early, late = slice(0, S // 2), slice(S // 2, S)
 
     with ExitStack() as ctx:
         keep = ctx.enter_context(tc.tile_pool(name="keep", bufs=1))
@@ -48,123 +50,132 @@ def tile_picked_modres_linrelu_lo_kernel(tc, xT, gate, res, w1, offs, out_0, out
         gate_cols = keep.tile([P, PACK], F32, name="gate_cols")
         x_planes = [keep.tile([P, T], F32, name="x_plane%d" % j, align_bytes=DMA_ALIGN) for j in range(PACK)]
         windows = [keep.tile([P, T], F32, name="window%d" % t, align_bytes=DMA_ALIGN) for t in range(PACK)]
-        w_ranges = ((0, W_EARLY), (W_EARLY, P))
-        w_parts = [keep.tile([P, PACK, PACK * (last - first)], F32, name="w_part%d" % first, tag="w_part%d" % first, align_bytes=DMA_ALIGN) for first, last in w_ranges]
+        w_halves = [keep.tile([P, PACK, N // 2], F32, name="w_half%d" % h, align_bytes=DMA_ALIGN) for h in range(2)]
         nc.sync.dma_start(x_planes[0][:], x_rows[:, 0, :])
         nc.sync.dma_start(offsets[:], offs)
+        nc.sync.dma_start(gate_cols[:], gate[0:1, :].rearrange("o (p c) -> p (o c)", c=PACK))
         for j in range(1, PACK):
             nc.sync.dma_start(x_planes[j][:], x_rows[:, j, :])
-        nc.sync.dma_start(w_parts[0][:], w_rows[:, :, 0:PACK * W_EARLY])
-        nc.sync.dma_start(gate_cols[:], gate[0:1, :].rearrange("o (p c) -> p (o c)", c=PACK))
-        nc.sync.dma_start(w_parts[1][:], w_rows[:, :, PACK * W_EARLY:N])
-        for t in RES_ORDER:
+        for h in range(2):
+            nc.sync.dma_start(w_halves[h][:], w_rows[:, :, h * N // 2:(h + 1) * N // 2])
+        for t in PLANE_ORDER:
             nc.sync.dma_start(windows[t][:], res_rows[:, t, :])
 
         warm_in = keep.tile([P, 1], F32, name="warm_in")
         warm_out = keep.tile([P, 1], F32, name="warm_out")
         nc.vector.memset(warm_in[:], 0.0)
         nc.scalar.activation(warm_out[:], warm_in[:], ACT.Copy)
+
         identity = keep.tile([P, P], F32, name="identity")
-        make_identity(nc, identity[:])
+        ones = keep.tile([P, QUAD], F32, name="ones", align_bytes=64)
+        column = keep.tile([P, QUAD], F32, name="column", align_bytes=64)
+        row = keep.tile([P, QUAD], F32, name="row", align_bytes=64)
+        nc.vector.memset(ones[:], 1.0)
+        nc.vector.memset(identity[:], 0.0)
+        nc.vector.tensor_tensor_scan(column[:], ones[:], ones[:], 0.0, ALU.add, ALU.mult)
+        nc.vector.transpose(row[:], column[:])
+        for first in range(0, P, QUAD):
+            block = slice(first, first + QUAD)
+            nc.vector.tensor_tensor(identity[block, block], column[block, :], row[block, :], ALU.is_equal)
         gate_ps = psum.tile([P, PACK, P], F32, name="gate_ps")
         for c in range(PACK):
             nc.tensor.transpose(gate_ps[:, c, :], gate_cols[:, c:c + 1].to_broadcast([P, P]), identity[:])
 
+        w_size = 2 * P * PACK
         x_grouped = keep.tile([P, S, PACK], BF16, name="x_grouped", align_bytes=64)
         x_plain = [keep.tile([P, 2, S], BF16, name="x_plain%d" % u, align_bytes=64) for u in range(2)]
-        whole = slice(0, S)
+        gate_sb = keep.tile([P, S], F32, name="gate_sb", align_bytes=64)
         nc.scalar.activation(x_plain[0][:, 0, :], picked(x_planes[0], whole), ACT.Copy)
+        nc.scalar.copy(gate_sb[:].rearrange("p (n c) -> p n c", c=PACK), gate_ps[:].rearrange("p c n -> p n c"))
         nc.vector.tensor_copy(x_plain[0][:, 1, :], picked(x_planes[1], whole))
         nc.scalar.activation(x_plain[1][:, 0, :], picked(x_planes[2], whole), ACT.Copy)
         nc.vector.tensor_copy(x_grouped[:, :, 0:2], x_plain[0][:].rearrange("p j s -> p s j"))
-        nc.vector.tensor_copy(x_plain[1][:, 1, halves[0]], picked(x_planes[3], halves[0]))
-        nc.scalar.activation(x_plain[1][:, 1, halves[1]], picked(x_planes[3], halves[1]), ACT.Copy)
-        for entries, copy in ((slice(0, X_SPLIT), nc.vector.tensor_copy), (slice(X_SPLIT, S), nc.scalar.copy)):
+        lower, upper = slice(0, X_SPLIT), slice(X_SPLIT, S)
+        nc.vector.tensor_copy(x_plain[1][:, 1, lower], picked(x_planes[3], lower))
+        nc.scalar.activation(x_plain[1][:, 1, upper], picked(x_planes[3], upper), ACT.Copy)
+        for entries, copy in ((lower, nc.vector.tensor_copy), (upper, nc.scalar.copy)):
             copy(x_grouped[:, entries, 2:PACK], x_plain[1][:, :, entries].rearrange("p j s -> p s j"))
+
+        even_rounded = keep.tile([P, w_size], BF16, name="even_rounded", tag="even_rounded", align_bytes=64)
+        odd_rounded = keep.tile([P, w_size], BF16, name="odd_rounded", align_bytes=64)
+        w_grouped = [tile[:].rearrange("p (t m j) -> p t m j", t=2, j=PACK) for tile in (even_rounded, odd_rounded)]
+
+        def round_w(copy, h, planes):
+            u, slots = planes.start % 2, slice(planes.start // 2, (planes.stop + 1) // 2)
+            copy(w_grouped[u][:, slots, h * P // 2:(h + 1) * P // 2, :].rearrange("p t m j -> p m j t"),
+                 w_halves[h][:].rearrange("p j (m t) -> p m j t", t=PACK)[:, :, :, planes])
+
         x_codes = keep.tile([P, S], U32, name="x_codes", align_bytes=64)
         x_scales = keep.tile([P, S], U8, name="x_scales", align_bytes=64)
         nc.vector.quantize_mx(out=x_codes[:].bitcast(FP8X4), scales=x_scales[:], in_=x_grouped[:].rearrange("p s j -> p (s j)"))
 
-        w_codes = {t: keep.tile([P, 2 * P], U32, name="w_codes%d" % t, align_bytes=64) for t in (0, 1)}
-        w_scales = {t: keep.tile([P, 2 * P], U8, name="w_scales%d" % t, align_bytes=64) for t in (0, 1)}
-        w_grouped = {t: keep.tile([P, 2, P, PACK], BF16, name="w_grouped%d" % t, tag="w_grouped%d" % t, align_bytes=64) for t in (0, 1)}
-        for part, t, copy in ((0, 0, nc.scalar.copy), (0, 1, nc.vector.tensor_copy), (1, 0, nc.scalar.copy), (1, 1, nc.scalar.copy)):
-            first, last = w_ranges[part]
-            copy(w_grouped[t][:, :, first:last, :].rearrange("p t m j -> p m j t"),
-                 w_parts[part][:].rearrange("p j (m t) -> p m j t", t=PACK)[:, :, :, t:PACK:2])
-        for t in (0, 1):
-            nc.vector.quantize_mx(out=w_codes[t][:].bitcast(FP8X4), scales=w_scales[t][:],
-                                  in_=w_grouped[t][:].rearrange("p t m j -> p (t m j)"))
-            if t == 0:
-                gate_sb = keep.tile([P, S], F32, name="gate_sb", tag="w_grouped0", align_bytes=64)
-                nc.vector.tensor_copy(gate_sb[:].rearrange("p (n c) -> p n c", c=PACK), gate_ps[:].rearrange("p c n -> p n c"))
+        round_w(nc.scalar.copy, 0, slice(0, 3, 2))
+        round_w(nc.vector.tensor_copy, 0, slice(1, 4, 2))
+        round_w(nc.scalar.copy, 1, slice(0, 3, 2))
+        round_w(nc.scalar.copy, 1, slice(1, 4, 2))
+        w_codes = [keep.tile([P, 2 * P], U32, name="w_codes%d" % u, align_bytes=64) for u in range(2)]
+        w_scales = {}
+        for u, planes in ((0, slice(0, 2)), (1, slice(0, 2))):
+            columns = slice(planes.start * P, planes.stop * P)
+            w_scales[u] = keep.tile([P, 2 * P], U8, name="w_scales%d" % u, tag=("w_scales0", "even_rounded")[u], align_bytes=64)
+            nc.vector.quantize_mx(out=w_codes[u][:, columns].bitcast(FP8X4), scales=w_scales[u][:, columns],
+                                  in_=w_grouped[u][:, planes].rearrange("p t m j -> p (t m j)"))
 
         gated = {}
-        for t in (0, 2, 1, 3):
+        for t in PLANE_ORDER:
             sums = psum.tile([P, S], F32, name="sums%d" % t)
-            pair, columns = t % 2, slice(t // 2 * P, (t // 2 + 1) * P)
-            nc.tensor.matmul_mx(out=sums[:], lhsT=w_codes[pair][:, columns].bitcast(FP8X4), lhsT_scale=w_scales[pair][:, columns],
+            u, columns = t % 2, slice(t // 2 * P, (t // 2 + 1) * P)
+            nc.tensor.matmul_mx(out=sums[:], lhsT=w_codes[u][:, columns].bitcast(FP8X4), lhsT_scale=w_scales[u][:, columns],
                                 rhs=x_codes[:].bitcast(FP8X4), rhs_scale=x_scales[:], start=True, stop=True)
             gated[t] = keep.tile([P, S], F32, name="gated%d" % t, tag="gated%d" % t, align_bytes=64)
             nc.vector.scalar_tensor_tensor(gated[t][:], sums[:], 0.0, gate_sb[:], ALU.max, ALU.mult)
 
-        early, late = halves
-        updates = {t: keep.tile([P, S], F32, name="update%d" % t, tag="update%d" % t, align_bytes=64) for t in range(PACK)}
-        old0 = keep.tile([P, S], F32, name="old0")
-        old2 = keep.tile([P, S // 2], F32, name="old2")
-        old3 = keep.tile([P, S], F32, name="old3", tag="old3", align_bytes=64)
-        olds = {(2, 0): old2[:], (2, 1): updates[3][:, late], (3, 0): old3[:, early], (3, 1): old3[:, late],
-                (1, 0): updates[3][:, early], (1, 1): updates[2][:, late]}
-        nc.scalar.activation(old0[:], picked(windows[0], whole), ACT.Copy)
-        for t in RES_ORDER[1:]:
-            for half, entries in enumerate(halves):
-                if (t, half) == (3, 0):
-                    nc.vector.tensor_copy(olds[t, half], picked(windows[t], entries))
-                else:
-                    nc.scalar.activation(olds[t, half], picked(windows[t], entries), ACT.Copy)
-        between, rest = slice(0, BETWEEN), slice(BETWEEN, S)
-        nc.gpsimd.tensor_tensor(updates[0][:], gated[0][:], old0[:], ALU.add)
-        for t, entries, old in ((2, early, olds[2, 0]), (1, early, olds[1, 0]), (3, between, old3[:, between]),
-                                (1, late, olds[1, 1]), (2, late, olds[2, 1]), (3, rest, old3[:, rest])):
-            nc.gpsimd.tensor_tensor(updates[t][:, entries], gated[t][:, entries], old, ALU.add)
+        lead, shared, after_lead = slice(0, SHARE), slice(SHARE, 2 * SHARE), slice(SHARE, S)
+        old1_update3 = keep.tile([P, S + SHARE], F32, name="old1_update3", align_bytes=64)
+        old3_update2 = keep.tile([P, S + S // 2], F32, name="old3_update2", align_bytes=64)
+        updates = {t: keep.tile([P, S], F32, name="update%d" % t, align_bytes=64)[:] for t in (0, 1)}
+        updates.update({2: old3_update2[:, S // 2:], 3: old1_update3[:, 0:S]})
+        olds = {t: keep.tile([P, S], F32, name="old%d" % t, tag="old%d" % t, align_bytes=64)[:] for t in (0, 2)}
+        olds.update({1: old1_update3[:, SHARE:], 3: old3_update2[:, 0:S]})
+        for t, entries in ((0, whole), (2, whole), (3, whole), (1, lead), (1, after_lead)):
+            nc.scalar.activation(olds[t][:, entries], picked(windows[t], entries), ACT.Copy)
+        for t, entries in ((0, whole), (2, late), (1, lead), (3, early), (1, after_lead), (3, late), (2, early)):
+            nc.gpsimd.tensor_tensor(updates[t][:, entries], gated[t][:, entries], olds[t][:, entries], ALU.add)
 
-        nc.vector.tensor_copy(picked(windows[0], whole), updates[0][:])
-        for t, entries in ((1, early), (3, between), (1, late), (3, rest)):
-            nc.scalar.activation(picked(windows[t], entries), updates[t][:, entries], ACT.Copy)
-        nc.vector.tensor_copy(picked(windows[2], whole), updates[2][:])
+        for engine, t, entries in (("vector", 0, whole), ("scalar", 1, lead), ("scalar", 3, lead), ("scalar", 1, after_lead),
+                                   ("vector", 3, shared), ("vector", 2, whole), ("scalar", 3, late)):
+            if engine == "vector":
+                nc.vector.tensor_copy(picked(windows[t], entries), updates[t][:, entries])
+            else:
+                nc.scalar.activation(picked(windows[t], entries), updates[t][:, entries], ACT.Copy)
 
-        sides = (slice(0, PIECE), slice(PIECE, T))
-        pairs = [keep.tile([P, 2, side.stop - side.start, 2], BF16, name="pairs_" + tag, tag=tag, align_bytes=64)
-                 for side, tag in zip(sides, ("update2", "old3"))]
-        for t in range(PACK):
+        pairs = keep.tile([P, T // BLOCK, 2, BLOCK, 2], BF16, name="pairs", tag="old2", align_bytes=64)
+
+        def in_blocks(t, blocks):
+            return windows[t][:].rearrange("p (n c) -> p n c", c=BLOCK)[:, blocks, :]
+
+        for t in (0, 1, 3, 2):
             nc.sync.dma_start(out_rows[:, t, :], windows[t][:])
-            for side, pair in zip(sides, pairs):
-                if t < 2 and side.start:
-                    nc.gpsimd.tensor_scalar(pair[:, 0, :, t], windows[t][:, side], 1.0, -0.0, ALU.mult, ALU.add)
-                else:
-                    nc.vector.tensor_copy(pair[:, t // 2, :, t % 2], windows[t][:, side])
-
-        pieces = [slice(first, first + PIECE) for first in range(0, T, PIECE)]
+        for t in range(2):
+            nc.gpsimd.tensor_scalar(pairs[:, :, 0, :, t], in_blocks(t, slice(0, T // BLOCK)), 1.0, -0.0, ALU.mult, ALU.add)
+        shares = ((nc.vector.tensor_copy, I32, VECTOR_PIECES), (nc.scalar.copy, U32, SCALAR_PIECES))
+        for copy, word, pieces in shares:
+            blocks = slice(pieces[0].start, pieces[-1].stop)
+            copy(pairs[:, blocks, 1, :, 1], in_blocks(3, blocks))
+            for blocks in pieces:
+                copy(pairs[:, blocks, 1, :, 0], in_blocks(2, blocks))
+        groups = []
+        for copy, word, pieces in shares:
+            words = pairs[:].rearrange("p n u c e -> p (n u c e)").bitcast(word).rearrange("p (n u c) -> p n c u", u=2, c=BLOCK)
+            for blocks in pieces:
+                group = keep.tile([P, (blocks.stop - blocks.start) * BLOCK * PACK], BF16, name="out_grouped%d" % blocks.start, align_bytes=64)
+                copy(group[:].bitcast(word).rearrange("p (n c u) -> p n c u", u=2, c=BLOCK), words[:, blocks])
+                groups.append((slice(blocks.start * BLOCK, blocks.stop * BLOCK), group))
         y_scales = keep.tile([P, T], U8, name="y_scales", align_bytes=DMA_ALIGN)
-        groups = [keep.tile([P, PIECE * PACK], BF16, name="out_grouped%d" % n, align_bytes=64) for n in range(len(pieces))]
-
-        def weave(n, copy, word):
-            side = min(n, 1)
-            first = pieces[n].start - sides[side].start
-            words = pairs[side][:].rearrange("p u c e -> p (u c e)").bitcast(word).rearrange("p (u c) -> p c u", u=2)
-            copy(groups[n][:].bitcast(word).rearrange("p (c u) -> p c u", u=2), words[:, first:first + PIECE, :])
-
-        def quantise(n):
-            y_codes = keep.tile([P, PIECE], U32, name="y_codes%d" % n, align_bytes=DMA_ALIGN)
-            nc.vector.quantize_mx(out=y_codes[:].bitcast(FP8X4), scales=y_scales[:, pieces[n]], in_=groups[n][:])
-            nc.sync.dma_start(out_words[:, pieces[n]], y_codes[:].bitcast(I32))
-
-        for n in range(3):
-            weave(n, nc.scalar.copy, U32)
-        quantise(0)
-        weave(3, nc.vector.tensor_copy, I32)
-        for n in (1, 3, 2):
-            quantise(n)
-        for row in range(4):
-            queue = nc.scalar if row % 2 else nc.sync
-            queue.dma_start(out_scales[row:16:4, :], y_scales[row:P:32, :].bitcast(I32))
+        for columns, group in groups:
+            y_codes = keep.tile([P, columns.stop - columns.start], U32, name="y_codes%d" % columns.start, align_bytes=DMA_ALIGN)
+            nc.vector.quantize_mx(out=y_codes[:].bitcast(FP8X4), scales=y_scales[:, columns], in_=group[:])
+            nc.sync.dma_start(out_words[:, columns], y_codes[:].bitcast(I32))
+        for first in range(4):
+            queue = nc.scalar if first % 2 else nc.sync
+            queue.dma_start(out_scales[first:16:4, :], y_scales[first:P:QUAD, :].bitcast(I32))

@@ -8,9 +8,13 @@ PACK = 4
 QUAD = 32
 FLOPS = 2 * K * S * N
 
-PLANE_ORDER = (0, 2, 3, 1)
-X_SPLIT = 320
+PRODUCT_ORDER = (0, 2, 1, 3)
+RES_ORDER = (0, 2, 3, 1)
+X_SPLIT = 352
+RES_SPLIT = 128
 SHARE = 128
+HELD = 64
+VECTOR_ONLY = 2
 BLOCK = 64
 VECTOR_PIECES = (slice(0, 6), slice(6, 10))
 SCALAR_PIECES = (slice(10, 14), slice(14, 16))
@@ -36,7 +40,6 @@ def tile_picked_modres_linrelu_lo_kernel(tc, xT, gate, res, w1, offs, out_0, out
     out_words = out_1.rearrange("z p c r -> p (z c r)").bitcast(I32)
     out_scales = out_2.rearrange("z q c -> q (z c)").bitcast(I32)
     whole = slice(0, S)
-    early, late = slice(0, S // 2), slice(S // 2, S)
 
     with ExitStack() as ctx:
         keep = ctx.enter_context(tc.tile_pool(name="keep", bufs=1))
@@ -50,15 +53,18 @@ def tile_picked_modres_linrelu_lo_kernel(tc, xT, gate, res, w1, offs, out_0, out
         gate_cols = keep.tile([P, PACK], F32, name="gate_cols")
         x_planes = [keep.tile([P, T], F32, name="x_plane%d" % j, align_bytes=DMA_ALIGN) for j in range(PACK)]
         windows = [keep.tile([P, T], F32, name="window%d" % t, align_bytes=DMA_ALIGN) for t in range(PACK)]
-        w_halves = [keep.tile([P, PACK, N // 2], F32, name="w_half%d" % h, align_bytes=DMA_ALIGN) for h in range(2)]
+        half_size = PACK * N // 2
+        w_early = keep.tile([P, half_size], F32, name="w_early", align_bytes=DMA_ALIGN)
+        w_late_old0 = keep.tile([P, half_size + S - RES_SPLIT], F32, name="w_late_old0", align_bytes=DMA_ALIGN)
+        w_halves = [tile[:, 0:half_size].rearrange("p (j c) -> p j c", j=PACK) for tile in (w_early, w_late_old0)]
         nc.sync.dma_start(x_planes[0][:], x_rows[:, 0, :])
         nc.sync.dma_start(offsets[:], offs)
         nc.sync.dma_start(gate_cols[:], gate[0:1, :].rearrange("o (p c) -> p (o c)", c=PACK))
         for j in range(1, PACK):
             nc.sync.dma_start(x_planes[j][:], x_rows[:, j, :])
         for h in range(2):
-            nc.sync.dma_start(w_halves[h][:], w_rows[:, :, h * N // 2:(h + 1) * N // 2])
-        for t in PLANE_ORDER:
+            nc.sync.dma_start(w_halves[h], w_rows[:, :, h * N // 2:(h + 1) * N // 2])
+        for t in RES_ORDER:
             nc.sync.dma_start(windows[t][:], res_rows[:, t, :])
 
         warm_in = keep.tile([P, 1], F32, name="warm_in")
@@ -83,18 +89,16 @@ def tile_picked_modres_linrelu_lo_kernel(tc, xT, gate, res, w1, offs, out_0, out
 
         w_size = 2 * P * PACK
         x_grouped = keep.tile([P, S, PACK], BF16, name="x_grouped", align_bytes=64)
-        x_plain = [keep.tile([P, 2, S], BF16, name="x_plain%d" % u, align_bytes=64) for u in range(2)]
+        x_plain = keep.tile([P, PACK, S - X_SPLIT], BF16, name="x_plain", align_bytes=64)
         gate_sb = keep.tile([P, S], F32, name="gate_sb", align_bytes=64)
-        nc.scalar.activation(x_plain[0][:, 0, :], picked(x_planes[0], whole), ACT.Copy)
-        nc.scalar.copy(gate_sb[:].rearrange("p (n c) -> p n c", c=PACK), gate_ps[:].rearrange("p c n -> p n c"))
-        nc.vector.tensor_copy(x_plain[0][:, 1, :], picked(x_planes[1], whole))
-        nc.scalar.activation(x_plain[1][:, 0, :], picked(x_planes[2], whole), ACT.Copy)
-        nc.vector.tensor_copy(x_grouped[:, :, 0:2], x_plain[0][:].rearrange("p j s -> p s j"))
         lower, upper = slice(0, X_SPLIT), slice(X_SPLIT, S)
-        nc.vector.tensor_copy(x_plain[1][:, 1, lower], picked(x_planes[3], lower))
-        nc.scalar.activation(x_plain[1][:, 1, upper], picked(x_planes[3], upper), ACT.Copy)
-        for entries, copy in ((lower, nc.vector.tensor_copy), (upper, nc.scalar.copy)):
-            copy(x_grouped[:, entries, 2:PACK], x_plain[1][:, :, entries].rearrange("p j s -> p s j"))
+        for j in range(PACK):
+            nc.vector.tensor_copy(x_grouped[:, lower, j], picked(x_planes[j], lower))
+            nc.scalar.activation(x_plain[:, j, :], picked(x_planes[j], upper), ACT.Copy)
+            if j == 0:
+                nc.scalar.copy(gate_sb[:].rearrange("p (n c) -> p n c", c=PACK), gate_ps[:].rearrange("p c n -> p n c"))
+            if j % 2:
+                nc.scalar.copy(x_grouped[:, upper, j - 1:j + 1], x_plain[:, j - 1:j + 1, :].rearrange("p j s -> p s j"))
 
         even_rounded = keep.tile([P, w_size], BF16, name="even_rounded", tag="even_rounded", align_bytes=64)
         odd_rounded = keep.tile([P, w_size], BF16, name="odd_rounded", align_bytes=64)
@@ -103,26 +107,29 @@ def tile_picked_modres_linrelu_lo_kernel(tc, xT, gate, res, w1, offs, out_0, out
         def round_w(copy, h, planes):
             u, slots = planes.start % 2, slice(planes.start // 2, (planes.stop + 1) // 2)
             copy(w_grouped[u][:, slots, h * P // 2:(h + 1) * P // 2, :].rearrange("p t m j -> p m j t"),
-                 w_halves[h][:].rearrange("p j (m t) -> p m j t", t=PACK)[:, :, :, planes])
+                 w_halves[h].rearrange("p j (m t) -> p m j t", t=PACK)[:, :, :, planes])
 
         x_codes = keep.tile([P, S], U32, name="x_codes", align_bytes=64)
         x_scales = keep.tile([P, S], U8, name="x_scales", align_bytes=64)
         nc.vector.quantize_mx(out=x_codes[:].bitcast(FP8X4), scales=x_scales[:], in_=x_grouped[:].rearrange("p s j -> p (s j)"))
 
         round_w(nc.scalar.copy, 0, slice(0, 3, 2))
-        round_w(nc.vector.tensor_copy, 0, slice(1, 4, 2))
-        round_w(nc.scalar.copy, 1, slice(0, 3, 2))
-        round_w(nc.scalar.copy, 1, slice(1, 4, 2))
+        round_w(nc.scalar.copy, 0, slice(1, 4, 2))
+        round_w(nc.vector.tensor_copy, 1, slice(0, 3, 2))
+        round_w(nc.vector.tensor_copy, 1, slice(1, 4, 2))
         w_codes = [keep.tile([P, 2 * P], U32, name="w_codes%d" % u, align_bytes=64) for u in range(2)]
-        w_scales = {}
-        for u, planes in ((0, slice(0, 2)), (1, slice(0, 2))):
+        w_scales = {0: keep.tile([P, 2 * P], U8, name="w_scales0", align_bytes=64)}
+        for u, planes in ((0, slice(0, 1)), (0, slice(1, 2)), (1, slice(0, 2))):
             columns = slice(planes.start * P, planes.stop * P)
-            w_scales[u] = keep.tile([P, 2 * P], U8, name="w_scales%d" % u, tag=("w_scales0", "even_rounded")[u], align_bytes=64)
+            if u:
+                w_scales[u] = keep.tile([P, 2 * P], U8, name="w_scales1", tag="even_rounded", align_bytes=64)
             nc.vector.quantize_mx(out=w_codes[u][:, columns].bitcast(FP8X4), scales=w_scales[u][:, columns],
                                   in_=w_grouped[u][:, planes].rearrange("p t m j -> p (t m j)"))
 
+        old0 = w_late_old0[:, half_size - RES_SPLIT:]
+        nc.vector.tensor_copy(old0[:, 0:RES_SPLIT], picked(windows[0], slice(0, RES_SPLIT)))
         gated = {}
-        for t in PLANE_ORDER:
+        for t in PRODUCT_ORDER:
             sums = psum.tile([P, S], F32, name="sums%d" % t)
             u, columns = t % 2, slice(t // 2 * P, (t // 2 + 1) * P)
             nc.tensor.matmul_mx(out=sums[:], lhsT=w_codes[u][:, columns].bitcast(FP8X4), lhsT_scale=w_scales[u][:, columns],
@@ -130,52 +137,60 @@ def tile_picked_modres_linrelu_lo_kernel(tc, xT, gate, res, w1, offs, out_0, out
             gated[t] = keep.tile([P, S], F32, name="gated%d" % t, tag="gated%d" % t, align_bytes=64)
             nc.vector.scalar_tensor_tensor(gated[t][:], sums[:], 0.0, gate_sb[:], ALU.max, ALU.mult)
 
-        lead, shared, after_lead = slice(0, SHARE), slice(SHARE, 2 * SHARE), slice(SHARE, S)
-        old1_update3 = keep.tile([P, S + SHARE], F32, name="old1_update3", align_bytes=64)
-        old3_update2 = keep.tile([P, S + S // 2], F32, name="old3_update2", align_bytes=64)
+        lead, after_lead = slice(0, SHARE), slice(SHARE, S)
+        most, held = slice(0, S - HELD), slice(S - HELD, S)
+        pairs_first = S - VECTOR_ONLY * 2 * BLOCK
+        chain = keep.tile([P, pairs_first + 2 * T], F32, name="chain", align_bytes=64)
+        old1_update3 = keep.tile([P, S], F32, name="old1_update3", align_bytes=64)
         updates = {t: keep.tile([P, S], F32, name="update%d" % t, align_bytes=64)[:] for t in (0, 1)}
-        updates.update({2: old3_update2[:, S // 2:], 3: old1_update3[:, 0:S]})
-        olds = {t: keep.tile([P, S], F32, name="old%d" % t, tag="old%d" % t, align_bytes=64)[:] for t in (0, 2)}
-        olds.update({1: old1_update3[:, SHARE:], 3: old3_update2[:, 0:S]})
-        for t, entries in ((0, whole), (2, whole), (3, whole), (1, lead), (1, after_lead)):
+        updates.update({2: chain[:, 0:S], 3: old1_update3[:]})
+        old2 = keep.tile([P, S], F32, name="old2", align_bytes=64)
+        olds = {0: old0, 1: old1_update3[:], 2: old2[:], 3: chain[:, held.start:held.start + S]}
+        for t, entries in ((0, slice(RES_SPLIT, S)), (2, whole), (3, whole), (1, lead), (1, after_lead)):
             nc.scalar.activation(olds[t][:, entries], picked(windows[t], entries), ACT.Copy)
-        for t, entries in ((0, whole), (2, late), (1, lead), (3, early), (1, after_lead), (3, late), (2, early)):
+        for t, entries in ((0, whole), (2, most), (1, lead), (1, after_lead), (3, lead), (2, held), (3, after_lead)):
             nc.gpsimd.tensor_tensor(updates[t][:, entries], gated[t][:, entries], olds[t][:, entries], ALU.add)
 
-        for engine, t, entries in (("vector", 0, whole), ("scalar", 1, lead), ("scalar", 3, lead), ("scalar", 1, after_lead),
-                                   ("vector", 3, shared), ("vector", 2, whole), ("scalar", 3, late)):
+        for engine, t, entries in (("vector", 0, whole), ("scalar", 1, lead), ("scalar", 1, after_lead),
+                                   ("vector", 3, lead), ("vector", 2, whole), ("scalar", 3, after_lead)):
             if engine == "vector":
                 nc.vector.tensor_copy(picked(windows[t], entries), updates[t][:, entries])
             else:
                 nc.scalar.activation(picked(windows[t], entries), updates[t][:, entries], ACT.Copy)
 
-        pairs = keep.tile([P, T // BLOCK, 2, BLOCK, 2], BF16, name="pairs", tag="old2", align_bytes=64)
+        pairs = chain[:, pairs_first:].bitcast(BF16).rearrange("p (n u c e) -> p n u c e", u=2, c=BLOCK, e=2)
 
         def in_blocks(t, blocks):
             return windows[t][:].rearrange("p (n c) -> p n c", c=BLOCK)[:, blocks, :]
 
-        for t in (0, 1, 3, 2):
+        for t in range(PACK):
             nc.sync.dma_start(out_rows[:, t, :], windows[t][:])
         for t in range(2):
-            nc.gpsimd.tensor_scalar(pairs[:, :, 0, :, t], in_blocks(t, slice(0, T // BLOCK)), 1.0, -0.0, ALU.mult, ALU.add)
+            blocks = slice(VECTOR_ONLY, T // BLOCK)
+            nc.gpsimd.tensor_scalar(pairs[:, blocks, 0, :, t], in_blocks(t, blocks), 1.0, -0.0, ALU.mult, ALU.add)
+            blocks = slice(0, VECTOR_ONLY)
+            nc.vector.tensor_copy(pairs[:, blocks, 0, :, t], in_blocks(t, blocks))
         shares = ((nc.vector.tensor_copy, I32, VECTOR_PIECES), (nc.scalar.copy, U32, SCALAR_PIECES))
         for copy, word, pieces in shares:
             blocks = slice(pieces[0].start, pieces[-1].stop)
-            copy(pairs[:, blocks, 1, :, 1], in_blocks(3, blocks))
+            copy(pairs[:, blocks, 1, :, 0], in_blocks(2, blocks))
             for blocks in pieces:
-                copy(pairs[:, blocks, 1, :, 0], in_blocks(2, blocks))
+                copy(pairs[:, blocks, 1, :, 1], in_blocks(3, blocks))
         groups = []
         for copy, word, pieces in shares:
-            words = pairs[:].rearrange("p n u c e -> p (n u c e)").bitcast(word).rearrange("p (n u c) -> p n c u", u=2, c=BLOCK)
+            words = chain[:, pairs_first:].bitcast(word).rearrange("p (n u c) -> p n c u", u=2, c=BLOCK)
             for blocks in pieces:
                 group = keep.tile([P, (blocks.stop - blocks.start) * BLOCK * PACK], BF16, name="out_grouped%d" % blocks.start, align_bytes=64)
                 copy(group[:].bitcast(word).rearrange("p (n c u) -> p n c u", u=2, c=BLOCK), words[:, blocks])
                 groups.append((slice(blocks.start * BLOCK, blocks.stop * BLOCK), group))
         y_scales = keep.tile([P, T], U8, name="y_scales", align_bytes=DMA_ALIGN)
+        y_codes = keep.tile([P, T], U32, name="y_codes", align_bytes=DMA_ALIGN)
+        stored = 0
         for columns, group in groups:
-            y_codes = keep.tile([P, columns.stop - columns.start], U32, name="y_codes%d" % columns.start, align_bytes=DMA_ALIGN)
-            nc.vector.quantize_mx(out=y_codes[:].bitcast(FP8X4), scales=y_scales[:, columns], in_=group[:])
-            nc.sync.dma_start(out_words[:, columns], y_codes[:].bitcast(I32))
+            nc.vector.quantize_mx(out=y_codes[:, columns].bitcast(FP8X4), scales=y_scales[:, columns], in_=group[:])
+            if columns.start:
+                nc.sync.dma_start(out_words[:, stored:columns.stop], y_codes[:, stored:columns.stop].bitcast(I32))
+                stored = columns.stop
         for first in range(4):
             queue = nc.scalar if first % 2 else nc.sync
             queue.dma_start(out_scales[first:16:4, :], y_scales[first:P:QUAD, :].bitcast(I32))

@@ -12,9 +12,8 @@ PRODUCT_ORDER = (0, 2, 1, 3)
 RES_ORDER = (0, 2, 3, 1)
 X_SPLIT = 352
 RES_SPLIT = 128
-SHARE = 128
-HELD = 64
-VECTOR_ONLY = 2
+LEAD = 128
+VECTOR_ONLY = 6
 BLOCK = 64
 VECTOR_PIECES = (slice(0, 6), slice(6, 10))
 SCALAR_PIECES = (slice(10, 14), slice(14, 16))
@@ -128,8 +127,15 @@ def tile_picked_modres_linrelu_lo_kernel(tc, xT, gate, res, w1, offs, out_0, out
 
         old0 = w_late_old0[:, half_size - RES_SPLIT:]
         nc.vector.tensor_copy(old0[:, 0:RES_SPLIT], picked(windows[0], slice(0, RES_SPLIT)))
+        lead, after_lead = slice(0, LEAD), slice(LEAD, S)
+        most, last = slice(0, S - LEAD), slice(S - LEAD, S)
+        pair_size = 2 * T
+        chain = keep.tile([P, pair_size - BLOCK + S - LEAD], F32, name="chain", align_bytes=64)
+        old2 = chain[:, pair_size - last.start:pair_size + LEAD]
         gated = {}
         for t in PRODUCT_ORDER:
+            if t == 2:
+                nc.vector.tensor_copy(old2[:, 0:RES_SPLIT], picked(windows[2], slice(0, RES_SPLIT)))
             sums = psum.tile([P, S], F32, name="sums%d" % t)
             u, columns = t % 2, slice(t // 2 * P, (t // 2 + 1) * P)
             nc.tensor.matmul_mx(out=sums[:], lhsT=w_codes[u][:, columns].bitcast(FP8X4), lhsT_scale=w_scales[u][:, columns],
@@ -137,28 +143,28 @@ def tile_picked_modres_linrelu_lo_kernel(tc, xT, gate, res, w1, offs, out_0, out
             gated[t] = keep.tile([P, S], F32, name="gated%d" % t, tag="gated%d" % t, align_bytes=64)
             nc.vector.scalar_tensor_tensor(gated[t][:], sums[:], 0.0, gate_sb[:], ALU.max, ALU.mult)
 
-        lead, after_lead = slice(0, SHARE), slice(SHARE, S)
-        most, held = slice(0, S - HELD), slice(S - HELD, S)
-        pairs_first = S - VECTOR_ONLY * 2 * BLOCK
-        chain = keep.tile([P, pairs_first + 2 * T], F32, name="chain", align_bytes=64)
-        old1_update3 = keep.tile([P, S], F32, name="old1_update3", align_bytes=64)
-        updates = {t: keep.tile([P, S], F32, name="update%d" % t, align_bytes=64)[:] for t in (0, 1)}
-        updates.update({2: chain[:, 0:S], 3: old1_update3[:]})
-        old2 = keep.tile([P, S], F32, name="old2", align_bytes=64)
-        olds = {0: old0, 1: old1_update3[:], 2: old2[:], 3: chain[:, held.start:held.start + S]}
-        for t, entries in ((0, slice(RES_SPLIT, S)), (2, whole), (3, whole), (1, lead), (1, after_lead)):
-            nc.scalar.activation(olds[t][:, entries], picked(windows[t], entries), ACT.Copy)
-        for t, entries in ((0, whole), (2, most), (1, lead), (1, after_lead), (3, lead), (2, held), (3, after_lead)):
-            nc.gpsimd.tensor_tensor(updates[t][:, entries], gated[t][:, entries], olds[t][:, entries], ALU.add)
+        update0 = keep.tile([P, S], F32, name="update0", align_bytes=64)
+        update1 = keep.tile([P, S], F32, name="update1", align_bytes=64)
+        leads = keep.tile([P, LEAD], F32, name="leads", align_bytes=64)
+        update2, update3_rest = chain[:, 0:S], chain[:, pair_size - BLOCK:]
+        old1_rest, old3 = chain[:, last.start:2 * last.start], chain[:, 2 * last.start:2 * last.start + S]
+        for old, t, entries in ((old0[:, RES_SPLIT:], 0, slice(RES_SPLIT, S)), (old2[:, RES_SPLIT:], 2, slice(RES_SPLIT, S)),
+                                (old3, 3, whole), (leads[:], 1, lead), (old1_rest, 1, after_lead)):
+            nc.scalar.activation(old, picked(windows[t], entries), ACT.Copy)
+        for update, t, entries, old in ((update0[:], 0, whole, old0), (update2[:, most], 2, most, old2[:, most]),
+                                        (update1[:, lead], 1, lead, leads[:]), (leads[:], 3, lead, old3[:, lead]),
+                                        (update1[:, after_lead], 1, after_lead, old1_rest), (update2[:, last], 2, last, old2[:, last]),
+                                        (update3_rest, 3, after_lead, old3[:, after_lead])):
+            nc.gpsimd.tensor_tensor(update, gated[t][:, entries], old, ALU.add)
 
-        for engine, t, entries in (("vector", 0, whole), ("scalar", 1, lead), ("scalar", 1, after_lead),
-                                   ("vector", 3, lead), ("vector", 2, whole), ("scalar", 3, after_lead)):
-            if engine == "vector":
-                nc.vector.tensor_copy(picked(windows[t], entries), updates[t][:, entries])
-            else:
-                nc.scalar.activation(picked(windows[t], entries), updates[t][:, entries], ACT.Copy)
+        nc.vector.tensor_copy(picked(windows[0], whole), update0[:])
+        for t, entries, update in ((1, lead, update1[:, lead]), (3, lead, leads[:]),
+                                   (1, after_lead, update1[:, after_lead]), (3, after_lead, update3_rest)):
+            nc.scalar.activation(picked(windows[t], entries), update, ACT.Copy)
+        nc.vector.tensor_copy(picked(windows[2], whole), update2)
 
-        pairs = chain[:, pairs_first:].bitcast(BF16).rearrange("p (n u c e) -> p n u c e", u=2, c=BLOCK, e=2)
+        pair_words = chain[:, 0:pair_size]
+        pairs = pair_words.bitcast(BF16).rearrange("p (n u c e) -> p n u c e", u=2, c=BLOCK, e=2)
 
         def in_blocks(t, blocks):
             return windows[t][:].rearrange("p (n c) -> p n c", c=BLOCK)[:, blocks, :]
@@ -178,19 +184,16 @@ def tile_picked_modres_linrelu_lo_kernel(tc, xT, gate, res, w1, offs, out_0, out
                 copy(pairs[:, blocks, 1, :, 1], in_blocks(3, blocks))
         groups = []
         for copy, word, pieces in shares:
-            words = chain[:, pairs_first:].bitcast(word).rearrange("p (n u c) -> p n c u", u=2, c=BLOCK)
+            words = pair_words.bitcast(word).rearrange("p (n u c) -> p n c u", u=2, c=BLOCK)
             for blocks in pieces:
                 group = keep.tile([P, (blocks.stop - blocks.start) * BLOCK * PACK], BF16, name="out_grouped%d" % blocks.start, align_bytes=64)
                 copy(group[:].bitcast(word).rearrange("p (n c u) -> p n c u", u=2, c=BLOCK), words[:, blocks])
                 groups.append((slice(blocks.start * BLOCK, blocks.stop * BLOCK), group))
         y_scales = keep.tile([P, T], U8, name="y_scales", align_bytes=DMA_ALIGN)
         y_codes = keep.tile([P, T], U32, name="y_codes", align_bytes=DMA_ALIGN)
-        stored = 0
         for columns, group in groups:
             nc.vector.quantize_mx(out=y_codes[:, columns].bitcast(FP8X4), scales=y_scales[:, columns], in_=group[:])
-            if columns.start:
-                nc.sync.dma_start(out_words[:, stored:columns.stop], y_codes[:, stored:columns.stop].bitcast(I32))
-                stored = columns.stop
+            nc.sync.dma_start(out_words[:, columns], y_codes[:, columns].bitcast(I32))
         for first in range(4):
             queue = nc.scalar if first % 2 else nc.sync
             queue.dma_start(out_scales[first:16:4, :], y_scales[first:P:QUAD, :].bitcast(I32))

@@ -58,9 +58,10 @@ def tile_picked_modres_linrelu_lo_kernel(tc, xT, gate, res, w1, offs, out_0, out
         w_halves = [tile[:, 0:half_size].rearrange("p (j c) -> p j c", j=PACK) for tile in (w_early, w_late_old0)]
         nc.sync.dma_start(x_planes[0][:], x_rows[:, 0, :])
         nc.sync.dma_start(offsets[:], offs)
-        nc.sync.dma_start(gate_cols[:], gate[0:1, :].rearrange("o (p c) -> p (o c)", c=PACK))
         for j in range(1, PACK):
             nc.sync.dma_start(x_planes[j][:], x_rows[:, j, :])
+            if j == 1:
+                nc.sync.dma_start(gate_cols[:], gate[0:1, :].rearrange("o (p c) -> p (o c)", c=PACK))
         for h in range(2):
             nc.sync.dma_start(w_halves[h], w_rows[:, :, h * N // 2:(h + 1) * N // 2])
         for t in RES_ORDER:
@@ -94,7 +95,7 @@ def tile_picked_modres_linrelu_lo_kernel(tc, xT, gate, res, w1, offs, out_0, out
         for j in range(PACK):
             nc.vector.tensor_copy(x_grouped[:, lower, j], picked(x_planes[j], lower))
             nc.scalar.activation(x_plain[:, j, :], picked(x_planes[j], upper), ACT.Copy)
-            if j == 0:
+            if j == 2:
                 nc.scalar.copy(gate_sb[:].rearrange("p (n c) -> p n c", c=PACK), gate_ps[:].rearrange("p c n -> p n c"))
             if j % 2:
                 nc.scalar.copy(x_grouped[:, upper, j - 1:j + 1], x_plain[:, j - 1:j + 1, :].rearrange("p j s -> p s j"))
@@ -128,10 +129,10 @@ def tile_picked_modres_linrelu_lo_kernel(tc, xT, gate, res, w1, offs, out_0, out
         old0 = w_late_old0[:, half_size - RES_SPLIT:]
         nc.vector.tensor_copy(old0[:, 0:RES_SPLIT], picked(windows[0], slice(0, RES_SPLIT)))
         lead, after_lead = slice(0, LEAD), slice(LEAD, S)
-        most, last = slice(0, S - LEAD), slice(S - LEAD, S)
+        most, last = slice(0, S // 2), slice(S // 2, S)
         pair_size = 2 * T
         chain = keep.tile([P, pair_size - BLOCK + S - LEAD], F32, name="chain", align_bytes=64)
-        old2 = chain[:, pair_size - last.start:pair_size + LEAD]
+        old2 = chain[:, pair_size - S // 2:pair_size + S // 2]
         gated = {}
         for t in PRODUCT_ORDER:
             if t == 2:
@@ -147,7 +148,8 @@ def tile_picked_modres_linrelu_lo_kernel(tc, xT, gate, res, w1, offs, out_0, out
         update1 = keep.tile([P, S], F32, name="update1", align_bytes=64)
         leads = keep.tile([P, LEAD], F32, name="leads", align_bytes=64)
         update2, update3_rest = chain[:, 0:S], chain[:, pair_size - BLOCK:]
-        old1_rest, old3 = chain[:, last.start:2 * last.start], chain[:, 2 * last.start:2 * last.start + S]
+        old3_first = S // 2 + S - LEAD
+        old1_rest, old3 = chain[:, S // 2:old3_first], chain[:, old3_first:old3_first + S]
         for old, t, entries in ((old0[:, RES_SPLIT:], 0, slice(RES_SPLIT, S)), (old2[:, RES_SPLIT:], 2, slice(RES_SPLIT, S)),
                                 (old3, 3, whole), (leads[:], 1, lead), (old1_rest, 1, after_lead)):
             nc.scalar.activation(old, picked(windows[t], entries), ACT.Copy)

@@ -197,5 +197,4 @@ def tile_picked_modres_linrelu_lo_kernel(tc, xT, gate, res, w1, offs, out_0, out
             nc.vector.quantize_mx(out=y_codes[:, columns].bitcast(FP8X4), scales=y_scales[:, columns], in_=group[:])
             nc.sync.dma_start(out_words[:, columns], y_codes[:, columns].bitcast(I32))
         for first in range(4):
-            queue = nc.scalar if first % 2 else nc.sync
-            queue.dma_start(out_scales[first:16:4, :], y_scales[first:P:QUAD, :].bitcast(I32))
+            nc.sync.dma_start(out_scales[first:16:4, :], y_scales[first:P:QUAD, :].bitcast(I32))

@@ -8,15 +8,12 @@ PACK = 4
 QUAD = 32
 FLOPS = 2 * K * S * N
 
-PRODUCT_ORDER = (0, 2, 1, 3)
-RES_ORDER = (0, 2, 3, 1)
 X_SPLIT = 352
 RES_SPLIT = 128
-LEAD = 128
-VECTOR_ONLY = 6
-BLOCK = 64
-VECTOR_PIECES = (slice(0, 6), slice(6, 10))
-SCALAR_PIECES = (slice(10, 14), slice(14, 16))
+SPARE = 16
+VECTOR_ONLY = 128
+SCALAR_PIECES = (slice(0, 384), slice(384, 640), slice(640, 768))
+VECTOR_PIECE = slice(768, 1024)
 DMA_ALIGN = 256
 
 F32 = mybir.dt.float32
@@ -51,7 +48,7 @@ def tile_picked_modres_linrelu_lo_kernel(tc, xT, gate, res, w1, offs, out_0, out
 
         gate_cols = keep.tile([P, PACK], F32, name="gate_cols")
         x_planes = [keep.tile([P, T], F32, name="x_plane%d" % j, align_bytes=DMA_ALIGN) for j in range(PACK)]
-        windows = [keep.tile([P, T], F32, name="window%d" % t, align_bytes=DMA_ALIGN) for t in range(PACK)]
+        windows = [keep.tile([P, T + SPARE * (t == 1)], F32, name="window%d" % t, align_bytes=DMA_ALIGN) for t in range(PACK)]
         half_size = PACK * N // 2
         w_early = keep.tile([P, half_size], F32, name="w_early", align_bytes=DMA_ALIGN)
         w_late_old0 = keep.tile([P, half_size + S - RES_SPLIT], F32, name="w_late_old0", align_bytes=DMA_ALIGN)
@@ -64,8 +61,8 @@ def tile_picked_modres_linrelu_lo_kernel(tc, xT, gate, res, w1, offs, out_0, out
                 nc.sync.dma_start(gate_cols[:], gate[0:1, :].rearrange("o (p c) -> p (o c)", c=PACK))
         for h in range(2):
             nc.sync.dma_start(w_halves[h], w_rows[:, :, h * N // 2:(h + 1) * N // 2])
-        for t in RES_ORDER:
-            nc.sync.dma_start(windows[t][:], res_rows[:, t, :])
+        for t in range(PACK):
+            nc.sync.dma_start(windows[t][:, 0:T], res_rows[:, t, :])
 
         warm_in = keep.tile([P, 1], F32, name="warm_in")
         warm_out = keep.tile([P, 1], F32, name="warm_out")
@@ -78,6 +75,7 @@ def tile_picked_modres_linrelu_lo_kernel(tc, xT, gate, res, w1, offs, out_0, out
         row = keep.tile([P, QUAD], F32, name="row", align_bytes=64)
         nc.vector.memset(ones[:], 1.0)
         nc.vector.memset(identity[:], 0.0)
+        nc.vector.memset(windows[1][:, T:], 1.0)
         nc.vector.tensor_tensor_scan(column[:], ones[:], ones[:], 0.0, ALU.add, ALU.mult)
         nc.vector.transpose(row[:], column[:])
         for first in range(0, P, QUAD):
@@ -105,18 +103,17 @@ def tile_picked_modres_linrelu_lo_kernel(tc, xT, gate, res, w1, offs, out_0, out
         w_grouped = [tile[:].rearrange("p (t m j) -> p t m j", t=2, j=PACK) for tile in (even_rounded, odd_rounded)]
 
         def round_w(copy, h, planes):
-            u, slots = planes.start % 2, slice(planes.start // 2, (planes.stop + 1) // 2)
-            copy(w_grouped[u][:, slots, h * P // 2:(h + 1) * P // 2, :].rearrange("p t m j -> p m j t"),
+            copy(w_grouped[planes.start // 2][:, :, h * P // 2:(h + 1) * P // 2, :].rearrange("p t m j -> p m j t"),
                  w_halves[h].rearrange("p j (m t) -> p m j t", t=PACK)[:, :, :, planes])
 
         x_codes = keep.tile([P, S], U32, name="x_codes", align_bytes=64)
         x_scales = keep.tile([P, S], U8, name="x_scales", align_bytes=64)
         nc.vector.quantize_mx(out=x_codes[:].bitcast(FP8X4), scales=x_scales[:], in_=x_grouped[:].rearrange("p s j -> p (s j)"))
 
-        round_w(nc.scalar.copy, 0, slice(0, 3, 2))
-        round_w(nc.scalar.copy, 0, slice(1, 4, 2))
-        round_w(nc.vector.tensor_copy, 1, slice(0, 3, 2))
-        round_w(nc.vector.tensor_copy, 1, slice(1, 4, 2))
+        round_w(nc.scalar.copy, 0, slice(0, 2))
+        round_w(nc.scalar.copy, 0, slice(2, 4))
+        round_w(nc.vector.tensor_copy, 1, slice(0, 2))
+        round_w(nc.vector.tensor_copy, 1, slice(2, 4))
         w_codes = [keep.tile([P, 2 * P], U32, name="w_codes%d" % u, align_bytes=64) for u in range(2)]
         w_scales = {0: keep.tile([P, 2 * P], U8, name="w_scales0", align_bytes=64)}
         for u, planes in ((0, slice(0, 1)), (0, slice(1, 2)), (1, slice(0, 2))):
@@ -128,73 +125,66 @@ def tile_picked_modres_linrelu_lo_kernel(tc, xT, gate, res, w1, offs, out_0, out
 
         old0 = w_late_old0[:, half_size - RES_SPLIT:]
         nc.vector.tensor_copy(old0[:, 0:RES_SPLIT], picked(windows[0], slice(0, RES_SPLIT)))
-        lead, after_lead = slice(0, LEAD), slice(LEAD, S)
-        most, last = slice(0, S // 2), slice(S // 2, S)
-        pair_size = 2 * T
-        chain = keep.tile([P, pair_size - BLOCK + S - LEAD], F32, name="chain", align_bytes=64)
-        old2 = chain[:, pair_size - S // 2:pair_size + S // 2]
-        gated = {}
-        for t in PRODUCT_ORDER:
-            if t == 2:
-                nc.vector.tensor_copy(old2[:, 0:RES_SPLIT], picked(windows[2], slice(0, RES_SPLIT)))
+        pairs_first = 2 * S - VECTOR_ONLY
+        chain = keep.tile([P, pairs_first + 2 * T], F32, name="chain", align_bytes=64)
+        update12, old3, gated3 = chain[:, 0:2 * S], chain[:, 2 * S:3 * S], chain[:, 3 * S:4 * S]
+        gated0 = keep.tile([P, S], F32, name="gated0", align_bytes=64)
+        gated12 = keep.tile([P, 2 * S], F32, name="gated12", align_bytes=64)
+        old12 = keep.tile([P, 2 * S], F32, name="old12", align_bytes=64)
+        gated = (gated0[:], gated12[:, 0:S], gated12[:, S:2 * S], gated3)
+        for t in range(PACK):
+            if t == 1:
+                nc.vector.tensor_copy(old12[:, 0:RES_SPLIT], picked(windows[1], slice(0, RES_SPLIT)))
             sums = psum.tile([P, S], F32, name="sums%d" % t)
-            u, columns = t % 2, slice(t // 2 * P, (t // 2 + 1) * P)
+            u, columns = t // 2, slice(t % 2 * P, (t % 2 + 1) * P)
             nc.tensor.matmul_mx(out=sums[:], lhsT=w_codes[u][:, columns].bitcast(FP8X4), lhsT_scale=w_scales[u][:, columns],
                                 rhs=x_codes[:].bitcast(FP8X4), rhs_scale=x_scales[:], start=True, stop=True)
-            gated[t] = keep.tile([P, S], F32, name="gated%d" % t, tag="gated%d" % t, align_bytes=64)
-            nc.vector.scalar_tensor_tensor(gated[t][:], sums[:], 0.0, gate_sb[:], ALU.max, ALU.mult)
+            nc.vector.scalar_tensor_tensor(gated[t], sums[:], 0.0, gate_sb[:], ALU.max, ALU.mult)
 
         update0 = keep.tile([P, S], F32, name="update0", align_bytes=64)
-        update1 = keep.tile([P, S], F32, name="update1", align_bytes=64)
-        leads = keep.tile([P, LEAD], F32, name="leads", align_bytes=64)
-        update2, update3_rest = chain[:, 0:S], chain[:, pair_size - BLOCK:]
-        old3_first = S // 2 + S - LEAD
-        old1_rest, old3 = chain[:, S // 2:old3_first], chain[:, old3_first:old3_first + S]
-        for old, t, entries in ((old0[:, RES_SPLIT:], 0, slice(RES_SPLIT, S)), (old2[:, RES_SPLIT:], 2, slice(RES_SPLIT, S)),
-                                (old3, 3, whole), (leads[:], 1, lead), (old1_rest, 1, after_lead)):
+        update3 = keep.tile([P, S], F32, name="update3", align_bytes=64)
+        for old, t, entries in ((old0[:, RES_SPLIT:], 0, slice(RES_SPLIT, S)), (old12[:, RES_SPLIT:S], 1, slice(RES_SPLIT, S)),
+                                (old12[:, S:], 2, whole)):
             nc.scalar.activation(old, picked(windows[t], entries), ACT.Copy)
-        for update, t, entries, old in ((update0[:], 0, whole, old0), (update2[:, most], 2, most, old2[:, most]),
-                                        (update1[:, lead], 1, lead, leads[:]), (leads[:], 3, lead, old3[:, lead]),
-                                        (update1[:, after_lead], 1, after_lead, old1_rest), (update2[:, last], 2, last, old2[:, last]),
-                                        (update3_rest, 3, after_lead, old3[:, after_lead])):
-            nc.gpsimd.tensor_tensor(update, gated[t][:, entries], old, ALU.add)
+        nc.scalar.activation(old3, picked(windows[3], whole), ACT.Copy, scale=windows[1][:, T:T + 1])
+        nc.gpsimd.tensor_tensor(update0[:], gated0[:], old0, ALU.add)
+        for entries in (slice(0, S), slice(S, 2 * S)):
+            nc.gpsimd.tensor_tensor(update12[:, entries], gated12[:, entries], old12[:, entries], ALU.add)
+        nc.gpsimd.tensor_tensor(update3[:], gated3, old3, ALU.add)
 
         nc.vector.tensor_copy(picked(windows[0], whole), update0[:])
-        for t, entries, update in ((1, lead, update1[:, lead]), (3, lead, leads[:]),
-                                   (1, after_lead, update1[:, after_lead]), (3, after_lead, update3_rest)):
-            nc.scalar.activation(picked(windows[t], entries), update, ACT.Copy)
-        nc.vector.tensor_copy(picked(windows[2], whole), update2)
-
-        pair_words = chain[:, 0:pair_size]
-        pairs = pair_words.bitcast(BF16).rearrange("p (n u c e) -> p n u c e", u=2, c=BLOCK, e=2)
-
-        def in_blocks(t, blocks):
-            return windows[t][:].rearrange("p (n c) -> p n c", c=BLOCK)[:, blocks, :]
-
+        nc.scalar.activation(picked(windows[1], whole), update12[:, 0:S], ACT.Copy, scale=ones[:, 0:1])
+        nc.vector.tensor_copy(picked(windows[2], whole), update12[:, S:2 * S])
+        nc.scalar.activation(picked(windows[3], whole), update3[:], ACT.Copy, scale=ones[:, 0:1])
         for t in range(PACK):
-            nc.sync.dma_start(out_rows[:, t, :], windows[t][:])
+            nc.sync.dma_start(out_rows[:, t, :], windows[t][:, 0:T])
+
+        pair_words = chain[:, pairs_first:pairs_first + 2 * T]
+        pairs = pair_words.bitcast(BF16).rearrange("p (u c e) -> p u c e", u=2, e=2)
         for t in range(2):
-            blocks = slice(VECTOR_ONLY, T // BLOCK)
-            nc.gpsimd.tensor_scalar(pairs[:, blocks, 0, :, t], in_blocks(t, blocks), 1.0, -0.0, ALU.mult, ALU.add)
-            blocks = slice(0, VECTOR_ONLY)
-            nc.vector.tensor_copy(pairs[:, blocks, 0, :, t], in_blocks(t, blocks))
-        shares = ((nc.vector.tensor_copy, I32, VECTOR_PIECES), (nc.scalar.copy, U32, SCALAR_PIECES))
-        for copy, word, pieces in shares:
-            blocks = slice(pieces[0].start, pieces[-1].stop)
-            copy(pairs[:, blocks, 1, :, 0], in_blocks(2, blocks))
-            for blocks in pieces:
-                copy(pairs[:, blocks, 1, :, 1], in_blocks(3, blocks))
-        groups = []
-        for copy, word, pieces in shares:
-            words = pair_words.bitcast(word).rearrange("p (n u c) -> p n c u", u=2, c=BLOCK)
-            for blocks in pieces:
-                group = keep.tile([P, (blocks.stop - blocks.start) * BLOCK * PACK], BF16, name="out_grouped%d" % blocks.start, align_bytes=64)
-                copy(group[:].bitcast(word).rearrange("p (n c u) -> p n c u", u=2, c=BLOCK), words[:, blocks])
-                groups.append((slice(blocks.start * BLOCK, blocks.stop * BLOCK), group))
+            nc.gpsimd.tensor_scalar(pairs[:, 0, VECTOR_ONLY:, t], windows[t][:, VECTOR_ONLY:T], 1.0, -0.0, ALU.mult, ALU.add)
+            nc.vector.tensor_copy(pairs[:, 0, 0:VECTOR_ONLY, t], windows[t][:, 0:VECTOR_ONLY])
+        nc.vector.tensor_copy(pairs[:, 1, :, 0], windows[2][:])
+        for columns in (SCALAR_PIECES[0], VECTOR_PIECE, slice(SCALAR_PIECES[1].start, SCALAR_PIECES[2].stop)):
+            nc.vector.tensor_copy(pairs[:, 1, columns, 1], windows[3][:, columns])
+
+        def weave(copy, word, columns):
+            group = keep.tile([P, (columns.stop - columns.start) * PACK], BF16, name="out_grouped%d" % columns.start, align_bytes=64)
+            copy(group[:].bitcast(word).rearrange("p (c u) -> p c u", u=2), pair_words.bitcast(word).rearrange("p (u c) -> p c u", u=2)[:, columns])
+            return group
+
         y_scales = keep.tile([P, T], U8, name="y_scales", align_bytes=DMA_ALIGN)
         y_codes = keep.tile([P, T], U32, name="y_codes", align_bytes=DMA_ALIGN)
-        for columns, group in groups:
+
+        def quantise(columns, group):
             nc.vector.quantize_mx(out=y_codes[:, columns].bitcast(FP8X4), scales=y_scales[:, columns], in_=group[:])
             nc.sync.dma_start(out_words[:, columns], y_codes[:, columns].bitcast(I32))
+
+        groups = [weave(nc.scalar.copy, U32, columns) for columns in SCALAR_PIECES]
+        own = weave(nc.vector.tensor_copy, I32, VECTOR_PIECE)
+        quantise(SCALAR_PIECES[0], groups[0])
+        quantise(VECTOR_PIECE, own)
+        quantise(SCALAR_PIECES[1], groups[1])
+        quantise(SCALAR_PIECES[2], groups[2])
         for first in range(4):
             nc.sync.dma_start(out_scales[first:16:4, :], y_scales[first:P:QUAD, :].bitcast(I32))

@@ -11,9 +11,10 @@ FLOPS = 2 * K * S * N
 X_SPLIT = 352
 RES_SPLIT = 128
 SPARE = 16
+LEAD = 64
 VECTOR_ONLY = 128
-SCALAR_PIECES = (slice(0, 384), slice(384, 640), slice(640, 768))
-VECTOR_PIECE = slice(768, 1024)
+SCALAR_PIECES = (slice(0, 384), slice(640, 896), slice(896, 1024))
+VECTOR_PIECE = slice(384, 640)
 DMA_ALIGN = 256
 
 F32 = mybir.dt.float32
@@ -126,15 +127,15 @@ def tile_picked_modres_linrelu_lo_kernel(tc, xT, gate, res, w1, offs, out_0, out
         old0 = w_late_old0[:, half_size - RES_SPLIT:]
         nc.vector.tensor_copy(old0[:, 0:RES_SPLIT], picked(windows[0], slice(0, RES_SPLIT)))
         pairs_first = 2 * S - VECTOR_ONLY
-        chain = keep.tile([P, pairs_first + 2 * T], F32, name="chain", align_bytes=64)
+        own = SCALAR_PIECES[2]
+        update3_first = pairs_first + T + own.start
+        chain = keep.tile([P, update3_first + S], F32, name="chain", align_bytes=64)
         update12, old3, gated3 = chain[:, 0:2 * S], chain[:, 2 * S:3 * S], chain[:, 3 * S:4 * S]
         gated0 = keep.tile([P, S], F32, name="gated0", align_bytes=64)
         gated12 = keep.tile([P, 2 * S], F32, name="gated12", align_bytes=64)
         old12 = keep.tile([P, 2 * S], F32, name="old12", align_bytes=64)
         gated = (gated0[:], gated12[:, 0:S], gated12[:, S:2 * S], gated3)
         for t in range(PACK):
-            if t == 1:
-                nc.vector.tensor_copy(old12[:, 0:RES_SPLIT], picked(windows[1], slice(0, RES_SPLIT)))
             sums = psum.tile([P, S], F32, name="sums%d" % t)
             u, columns = t // 2, slice(t % 2 * P, (t % 2 + 1) * P)
             nc.tensor.matmul_mx(out=sums[:], lhsT=w_codes[u][:, columns].bitcast(FP8X4), lhsT_scale=w_scales[u][:, columns],
@@ -142,20 +143,21 @@ def tile_picked_modres_linrelu_lo_kernel(tc, xT, gate, res, w1, offs, out_0, out
             nc.vector.scalar_tensor_tensor(gated[t], sums[:], 0.0, gate_sb[:], ALU.max, ALU.mult)
 
         update0 = keep.tile([P, S], F32, name="update0", align_bytes=64)
-        update3 = keep.tile([P, S], F32, name="update3", align_bytes=64)
-        for old, t, entries in ((old0[:, RES_SPLIT:], 0, slice(RES_SPLIT, S)), (old12[:, RES_SPLIT:S], 1, slice(RES_SPLIT, S)),
+        update3 = chain[:, update3_first:]
+        for old, t, entries in ((old0[:, RES_SPLIT:], 0, slice(RES_SPLIT, S)), (old12[:, 0:S], 1, whole),
                                 (old12[:, S:], 2, whole)):
             nc.scalar.activation(old, picked(windows[t], entries), ACT.Copy)
-        nc.scalar.activation(old3, picked(windows[3], whole), ACT.Copy, scale=windows[1][:, T:T + 1])
+        nc.scalar.activation(old3[:, 0:LEAD], picked(windows[3], slice(0, LEAD)), ACT.Copy, scale=windows[1][:, T:T + 1])
+        nc.scalar.activation(old3[:, LEAD:], picked(windows[3], slice(LEAD, S)), ACT.Copy)
         nc.gpsimd.tensor_tensor(update0[:], gated0[:], old0, ALU.add)
         for entries in (slice(0, S), slice(S, 2 * S)):
             nc.gpsimd.tensor_tensor(update12[:, entries], gated12[:, entries], old12[:, entries], ALU.add)
-        nc.gpsimd.tensor_tensor(update3[:], gated3, old3, ALU.add)
+        nc.gpsimd.tensor_tensor(update3, gated3, old3, ALU.add)
 
         nc.vector.tensor_copy(picked(windows[0], whole), update0[:])
         nc.scalar.activation(picked(windows[1], whole), update12[:, 0:S], ACT.Copy, scale=ones[:, 0:1])
         nc.vector.tensor_copy(picked(windows[2], whole), update12[:, S:2 * S])
-        nc.scalar.activation(picked(windows[3], whole), update3[:], ACT.Copy, scale=ones[:, 0:1])
+        nc.scalar.activation(picked(windows[3], whole), update3, ACT.Copy, scale=ones[:, 0:1])
         for t in range(PACK):
             nc.sync.dma_start(out_rows[:, t, :], windows[t][:, 0:T])
 
@@ -164,8 +166,10 @@ def tile_picked_modres_linrelu_lo_kernel(tc, xT, gate, res, w1, offs, out_0, out
         for t in range(2):
             nc.gpsimd.tensor_scalar(pairs[:, 0, VECTOR_ONLY:, t], windows[t][:, VECTOR_ONLY:T], 1.0, -0.0, ALU.mult, ALU.add)
             nc.vector.tensor_copy(pairs[:, 0, 0:VECTOR_ONLY, t], windows[t][:, 0:VECTOR_ONLY])
-        nc.vector.tensor_copy(pairs[:, 1, :, 0], windows[2][:])
-        for columns in (SCALAR_PIECES[0], VECTOR_PIECE, slice(SCALAR_PIECES[1].start, SCALAR_PIECES[2].stop)):
+        nc.vector.tensor_copy(pairs[:, 1, 0:own.start, 0], windows[2][:, 0:own.start])
+        for t in (2, 3):
+            nc.scalar.copy(pairs[:, 1, own, t - 2], windows[t][:, own])
+        for columns in (SCALAR_PIECES[0], VECTOR_PIECE, SCALAR_PIECES[1]):
             nc.vector.tensor_copy(pairs[:, 1, columns, 1], windows[3][:, columns])
 
         def weave(copy, word, columns):
@@ -181,9 +185,9 @@ def tile_picked_modres_linrelu_lo_kernel(tc, xT, gate, res, w1, offs, out_0, out
             nc.sync.dma_start(out_words[:, columns], y_codes[:, columns].bitcast(I32))
 
         groups = [weave(nc.scalar.copy, U32, columns) for columns in SCALAR_PIECES]
-        own = weave(nc.vector.tensor_copy, I32, VECTOR_PIECE)
+        woven = weave(nc.vector.tensor_copy, I32, VECTOR_PIECE)
         quantise(SCALAR_PIECES[0], groups[0])
-        quantise(VECTOR_PIECE, own)
+        quantise(VECTOR_PIECE, woven)
         quantise(SCALAR_PIECES[1], groups[1])
         quantise(SCALAR_PIECES[2], groups[2])
         for first in range(4):

@@ -16,6 +16,8 @@ VECTOR_ONLY = 128
 SCALAR_PIECES = (slice(0, 384), slice(640, 896), slice(896, 1024))
 VECTOR_PIECE = slice(384, 640)
 DMA_ALIGN = 256
+REGION = 64 * 1024
+SLOT = 8 * 1024
 
 F32 = mybir.dt.float32
 BF16 = mybir.dt.bfloat16
@@ -40,6 +42,7 @@ def tile_picked_modres_linrelu_lo_kernel(tc, xT, gate, res, w1, offs, out_0, out
 
     with ExitStack() as ctx:
         keep = ctx.enter_context(tc.tile_pool(name="keep", bufs=1))
+        spread = ctx.enter_context(tc.tile_pool(name="spread", bufs=1))
         psum = ctx.enter_context(tc.psum_pool(name="psum", bufs=1))
 
         offsets = keep.tile([P, S // 16], U16, name="offsets")
@@ -48,11 +51,11 @@ def tile_picked_modres_linrelu_lo_kernel(tc, xT, gate, res, w1, offs, out_0, out
             return window[:].indirect(offsets[:, entries.start // 16:entries.stop // 16])
 
         gate_cols = keep.tile([P, PACK], F32, name="gate_cols")
-        x_planes = [keep.tile([P, T], F32, name="x_plane%d" % j, align_bytes=DMA_ALIGN) for j in range(PACK)]
-        windows = [keep.tile([P, T + SPARE * (t == 1)], F32, name="window%d" % t, align_bytes=DMA_ALIGN) for t in range(PACK)]
+        x_planes = [spread.tile([P, T], F32, name="x_plane%d" % j, align_bytes=DMA_ALIGN, offset=j % 3 * REGION + (3 + j // 3) * SLOT) for j in range(PACK)]
+        windows = [spread.tile([P, T + SPARE * (t == 1)], F32, name="window%d" % t, align_bytes=DMA_ALIGN, offset=t * REGION) for t in range(PACK)]
         half_size = PACK * N // 2
-        w_early = keep.tile([P, half_size], F32, name="w_early", align_bytes=DMA_ALIGN)
-        w_late_old0 = keep.tile([P, half_size + S - RES_SPLIT], F32, name="w_late_old0", align_bytes=DMA_ALIGN)
+        w_early = spread.tile([P, half_size], F32, name="w_early", align_bytes=DMA_ALIGN, offset=REGION + SLOT)
+        w_late_old0 = spread.tile([P, half_size + S - RES_SPLIT], F32, name="w_late_old0", align_bytes=DMA_ALIGN, offset=2 * REGION + SLOT)
         w_halves = [tile[:, 0:half_size].rearrange("p (j c) -> p j c", j=PACK) for tile in (w_early, w_late_old0)]
         nc.sync.dma_start(x_planes[0][:], x_rows[:, 0, :])
         nc.sync.dma_start(offsets[:], offs)
@@ -129,7 +132,7 @@ def tile_picked_modres_linrelu_lo_kernel(tc, xT, gate, res, w1, offs, out_0, out
         pairs_first = 2 * S - VECTOR_ONLY
         own = SCALAR_PIECES[2]
         update3_first = pairs_first + T + own.start
-        chain = keep.tile([P, update3_first + S], F32, name="chain", align_bytes=64)
+        chain = spread.tile([P, update3_first + S], F32, name="chain", align_bytes=DMA_ALIGN, offset=SLOT)
         update12, old3, gated3 = chain[:, 0:2 * S], chain[:, 2 * S:3 * S], chain[:, 3 * S:4 * S]
         gated0 = keep.tile([P, S], F32, name="gated0", align_bytes=64)
         gated12 = keep.tile([P, 2 * S], F32, name="gated12", align_bytes=64)

from contextlib import ExitStack

import concourse.mybir as mybir

K, T, S, N = 512, 1024, 512, 512
P = 128
PACK = 4
QUAD = 32
FLOPS = 2 * K * S * N

X_SPLIT = 352
RES_SPLIT = 128
SPARE = 16
LEAD = 64
VECTOR_ONLY = 128
SCALAR_PIECES = (slice(0, 384), slice(640, 896), slice(896, 1024))
VECTOR_PIECE = slice(384, 640)
DMA_ALIGN = 256
REGION = 64 * 1024
SLOT = 8 * 1024

F32 = mybir.dt.float32
BF16 = mybir.dt.bfloat16
I32 = mybir.dt.int32
U32 = mybir.dt.uint32
U16 = mybir.dt.uint16
U8 = mybir.dt.uint8
FP8X4 = mybir.dt.float8_e4m3fn_x4
ALU = mybir.AluOpType
ACT = mybir.ActivationFunctionType


def tile_picked_modres_linrelu_lo_kernel(tc, xT, gate, res, w1, offs, out_0, out_1, out_2):
    nc = tc.nc
    x_rows = xT.rearrange("(p j) c -> p j c", j=PACK)
    w_rows = w1.rearrange("(p j) c -> p j c", j=PACK)
    res_rows = res.rearrange("(p t) c -> p t c", t=PACK)
    out_rows = out_0.rearrange("(p t) c -> p t c", t=PACK)
    out_words = out_1.rearrange("z p c r -> p (z c r)").bitcast(I32)
    out_scales = out_2.rearrange("z q c -> q (z c)").bitcast(I32)
    whole = slice(0, S)

    with ExitStack() as ctx:
        keep = ctx.enter_context(tc.tile_pool(name="keep", bufs=1))
        spread = ctx.enter_context(tc.tile_pool(name="spread", bufs=1))
        psum = ctx.enter_context(tc.psum_pool(name="psum", bufs=1))

        offsets = keep.tile([P, S // 16], U16, name="offsets")

        def picked(window, entries):
            return window[:].indirect(offsets[:, entries.start // 16:entries.stop // 16])

        gate_cols = keep.tile([P, PACK], F32, name="gate_cols")
        x_planes = [spread.tile([P, T], F32, name="x_plane%d" % j, align_bytes=DMA_ALIGN, offset=j % 3 * REGION + (3 + j // 3) * SLOT) for j in range(PACK)]
        windows = [spread.tile([P, T + SPARE * (t == 1)], F32, name="window%d" % t, align_bytes=DMA_ALIGN, offset=t * REGION) for t in range(PACK)]
        half_size = PACK * N // 2
        w_early = spread.tile([P, half_size], F32, name="w_early", align_bytes=DMA_ALIGN, offset=REGION + SLOT)
        w_late_old0 = spread.tile([P, half_size + S - RES_SPLIT], F32, name="w_late_old0", align_bytes=DMA_ALIGN, offset=2 * REGION + SLOT)
        w_halves = [tile[:, 0:half_size].rearrange("p (j c) -> p j c", j=PACK) for tile in (w_early, w_late_old0)]
        nc.sync.dma_start(x_planes[0][:], x_rows[:, 0, :])
        nc.sync.dma_start(offsets[:], offs)
        for j in range(1, PACK):
            nc.sync.dma_start(x_planes[j][:], x_rows[:, j, :])
            if j == 1:
                nc.sync.dma_start(gate_cols[:], gate[0:1, :].rearrange("o (p c) -> p (o c)", c=PACK))
        for h in range(2):
            nc.sync.dma_start(w_halves[h], w_rows[:, :, h * N // 2:(h + 1) * N // 2])
        for t in range(PACK):
            nc.sync.dma_start(windows[t][:, 0:T], res_rows[:, t, :])

        warm_in = keep.tile([P, 1], F32, name="warm_in")
        warm_out = keep.tile([P, 1], F32, name="warm_out")
        nc.vector.memset(warm_in[:], 0.0)
        nc.scalar.activation(warm_out[:], warm_in[:], ACT.Copy)

        identity = keep.tile([P, P], F32, name="identity")
        ones = keep.tile([P, QUAD], F32, name="ones", align_bytes=64)
        column = keep.tile([P, QUAD], F32, name="column", align_bytes=64)
        row = keep.tile([P, QUAD], F32, name="row", align_bytes=64)
        nc.vector.memset(ones[:], 1.0)
        nc.vector.memset(identity[:], 0.0)
        nc.vector.memset(windows[1][:, T:], 1.0)
        nc.vector.tensor_tensor_scan(column[:], ones[:], ones[:], 0.0, ALU.add, ALU.mult)
        nc.vector.transpose(row[:], column[:])
        for first in range(0, P, QUAD):
            block = slice(first, first + QUAD)
            nc.vector.tensor_tensor(identity[block, block], column[block, :], row[block, :], ALU.is_equal)
        gate_ps = psum.tile([P, PACK, P], F32, name="gate_ps")
        for c in range(PACK):
            nc.tensor.transpose(gate_ps[:, c, :], gate_cols[:, c:c + 1].to_broadcast([P, P]), identity[:])

        w_size = 2 * P * PACK
        x_grouped = keep.tile([P, S, PACK], BF16, name="x_grouped", align_bytes=64)
        x_plain = keep.tile([P, PACK, S - X_SPLIT], BF16, name="x_plain", align_bytes=64)
        gate_sb = keep.tile([P, S], F32, name="gate_sb", align_bytes=64)
        lower, upper = slice(0, X_SPLIT), slice(X_SPLIT, S)
        for j in range(PACK):
            nc.vector.tensor_copy(x_grouped[:, lower, j], picked(x_planes[j], lower))
            nc.scalar.activation(x_plain[:, j, :], picked(x_planes[j], upper), ACT.Copy)
            if j == 2:
                nc.scalar.copy(gate_sb[:].rearrange("p (n c) -> p n c", c=PACK), gate_ps[:].rearrange("p c n -> p n c"))
            if j % 2:
                nc.scalar.copy(x_grouped[:, upper, j - 1:j + 1], x_plain[:, j - 1:j + 1, :].rearrange("p j s -> p s j"))

        even_rounded = keep.tile([P, w_size], BF16, name="even_rounded", tag="even_rounded", align_bytes=64)
        odd_rounded = keep.tile([P, w_size], BF16, name="odd_rounded", align_bytes=64)
        w_grouped = [tile[:].rearrange("p (t m j) -> p t m j", t=2, j=PACK) for tile in (even_rounded, odd_rounded)]

        def round_w(copy, h, planes):
            copy(w_grouped[planes.start // 2][:, :, h * P // 2:(h + 1) * P // 2, :].rearrange("p t m j -> p m j t"),
                 w_halves[h].rearrange("p j (m t) -> p m j t", t=PACK)[:, :, :, planes])

        x_codes = keep.tile([P, S], U32, name="x_codes", align_bytes=64)
        x_scales = keep.tile([P, S], U8, name="x_scales", align_bytes=64)
        nc.vector.quantize_mx(out=x_codes[:].bitcast(FP8X4), scales=x_scales[:], in_=x_grouped[:].rearrange("p s j -> p (s j)"))

        round_w(nc.scalar.copy, 0, slice(0, 2))
        round_w(nc.scalar.copy, 0, slice(2, 4))
        round_w(nc.vector.tensor_copy, 1, slice(0, 2))
        round_w(nc.vector.tensor_copy, 1, slice(2, 4))
        w_codes = [keep.tile([P, 2 * P], U32, name="w_codes%d" % u, align_bytes=64) for u in range(2)]
        w_scales = {0: keep.tile([P, 2 * P], U8, name="w_scales0", align_bytes=64)}
        for u, planes in ((0, slice(0, 1)), (0, slice(1, 2)), (1, slice(0, 2))):
            columns = slice(planes.start * P, planes.stop * P)
            if u:
                w_scales[u] = keep.tile([P, 2 * P], U8, name="w_scales1", tag="even_rounded", align_bytes=64)
            nc.vector.quantize_mx(out=w_codes[u][:, columns].bitcast(FP8X4), scales=w_scales[u][:, columns],
                                  in_=w_grouped[u][:, planes].rearrange("p t m j -> p (t m j)"))

        old0 = w_late_old0[:, half_size - RES_SPLIT:]
        nc.vector.tensor_copy(old0[:, 0:RES_SPLIT], picked(windows[0], slice(0, RES_SPLIT)))
        pairs_first = 2 * S - VECTOR_ONLY
        own = SCALAR_PIECES[2]
        update3_first = pairs_first + T + own.start
        chain = spread.tile([P, update3_first + S], F32, name="chain", align_bytes=DMA_ALIGN, offset=SLOT)
        update12, old3, gated3 = chain[:, 0:2 * S], chain[:, 2 * S:3 * S], chain[:, 3 * S:4 * S]
        gated0 = keep.tile([P, S], F32, name="gated0", align_bytes=64)
        gated12 = keep.tile([P, 2 * S], F32, name="gated12", align_bytes=64)
        old12 = keep.tile([P, 2 * S], F32, name="old12", align_bytes=64)
        gated = (gated0[:], gated12[:, 0:S], gated12[:, S:2 * S], gated3)
        for t in range(PACK):
            sums = psum.tile([P, S], F32, name="sums%d" % t)
            u, columns = t // 2, slice(t % 2 * P, (t % 2 + 1) * P)
            nc.tensor.matmul_mx(out=sums[:], lhsT=w_codes[u][:, columns].bitcast(FP8X4), lhsT_scale=w_scales[u][:, columns],
                                rhs=x_codes[:].bitcast(FP8X4), rhs_scale=x_scales[:], start=True, stop=True)
            nc.vector.scalar_tensor_tensor(gated[t], sums[:], 0.0, gate_sb[:], ALU.max, ALU.mult)

        update0 = keep.tile([P, S], F32, name="update0", align_bytes=64)
        update3 = chain[:, update3_first:]
        for old, t, entries in ((old0[:, RES_SPLIT:], 0, slice(RES_SPLIT, S)), (old12[:, 0:S], 1, whole),
                                (old12[:, S:], 2, whole)):
            nc.scalar.activation(old, picked(windows[t], entries), ACT.Copy)
        nc.scalar.activation(old3[:, 0:LEAD], picked(windows[3], slice(0, LEAD)), ACT.Copy, scale=windows[1][:, T:T + 1])
        nc.scalar.activation(old3[:, LEAD:], picked(windows[3], slice(LEAD, S)), ACT.Copy)
        nc.gpsimd.tensor_tensor(update0[:], gated0[:], old0, ALU.add)
        for entries in (slice(0, S), slice(S, 2 * S)):
            nc.gpsimd.tensor_tensor(update12[:, entries], gated12[:, entries], old12[:, entries], ALU.add)
        nc.gpsimd.tensor_tensor(update3, gated3, old3, ALU.add)

        nc.vector.tensor_copy(picked(windows[0], whole), update0[:])
        nc.scalar.activation(picked(windows[1], whole), update12[:, 0:S], ACT.Copy, scale=ones[:, 0:1])
        nc.vector.tensor_copy(picked(windows[2], whole), update12[:, S:2 * S])
        nc.scalar.activation(picked(windows[3], whole), update3, ACT.Copy, scale=ones[:, 0:1])
        for t in range(PACK):
            nc.sync.dma_start(out_rows[:, t, :], windows[t][:, 0:T])

        pair_words = chain[:, pairs_first:pairs_first + 2 * T]
        pairs = pair_words.bitcast(BF16).rearrange("p (u c e) -> p u c e", u=2, e=2)
        for t in range(2):
            nc.gpsimd.tensor_scalar(pairs[:, 0, VECTOR_ONLY:, t], windows[t][:, VECTOR_ONLY:T], 1.0, -0.0, ALU.mult, ALU.add)
            nc.vector.tensor_copy(pairs[:, 0, 0:VECTOR_ONLY, t], windows[t][:, 0:VECTOR_ONLY])
        nc.vector.tensor_copy(pairs[:, 1, 0:own.start, 0], windows[2][:, 0:own.start])
        for t in (2, 3):
            nc.scalar.copy(pairs[:, 1, own, t - 2], windows[t][:, own])
        for columns in (SCALAR_PIECES[0], VECTOR_PIECE, SCALAR_PIECES[1]):
            nc.vector.tensor_copy(pairs[:, 1, columns, 1], windows[3][:, columns])

        def weave(copy, word, columns):
            group = keep.tile([P, (columns.stop - columns.start) * PACK], BF16, name="out_grouped%d" % columns.start, align_bytes=64)
            copy(group[:].bitcast(word).rearrange("p (c u) -> p c u", u=2), pair_words.bitcast(word).rearrange("p (u c) -> p c u", u=2)[:, columns])
            return group

        y_scales = keep.tile([P, T], U8, name="y_scales", align_bytes=DMA_ALIGN)
        y_codes = keep.tile([P, T], U32, name="y_codes", align_bytes=DMA_ALIGN)

        def quantise(columns, group):
            nc.vector.quantize_mx(out=y_codes[:, columns].bitcast(FP8X4), scales=y_scales[:, columns], in_=group[:])
            nc.sync.dma_start(out_words[:, columns], y_codes[:, columns].bitcast(I32))

        groups = [weave(nc.scalar.copy, U32, columns) for columns in SCALAR_PIECES]
        woven = weave(nc.vector.tensor_copy, I32, VECTOR_PIECE)
        quantise(SCALAR_PIECES[0], groups[0])
        quantise(VECTOR_PIECE, woven)
        quantise(SCALAR_PIECES[1], groups[1])
        quantise(SCALAR_PIECES[2], groups[2])
        for first in range(4):
            nc.sync.dma_start(out_scales[first:16:4, :], y_scales[first:P:QUAD, :].bitcast(I32))
